import numpy as np
import ml_dtypes


def mxq(x, axis, fmt="e4m3"):
    dtype, down = {"e4m3": (ml_dtypes.float8_e4m3fn, 7), "e5m2": (ml_dtypes.float8_e5m2, 14)}[fmt]
    v = np.moveaxis(np.asarray(x, np.float32).astype(ml_dtypes.bfloat16).astype(np.float64), axis, -1)
    blocks = v.reshape(v.shape[:-1] + (-1, 32))
    amax = np.abs(blocks).max(-1, keepdims=True)
    byte = np.maximum(np.where(amax > 0, np.frexp(amax)[1] - 1 + 127, 0) - down, 1)
    scale = np.exp2(byte - 127.0)
    codes = (blocks / scale).astype(np.float32).astype(dtype).astype(np.float64)
    return np.moveaxis((codes * scale).reshape(v.shape), -1, axis)


WIDE = False


def mx_kscale(k):
    if not WIDE:
        return np.ones(k)
    levels = np.array([10, -10, 5, -5, 0])
    if k % 512:
        return np.exp2(np.random.permutation(np.resize(levels, k // 32))).repeat(32)
    a = np.empty((k // 512, 16))
    for p in range(k // 512):
        a[p, :8] = np.random.permutation(np.resize(levels, 8))
        for g in range(8):
            far = levels[np.abs(levels - a[p, g]) >= 10]
            a[p, g + 8] = far[np.random.randint(len(far))]
    return np.exp2(a.ravel()).repeat(32)


def f64(x):
    return np.asarray(x).astype(np.float64)


def striped(idx):
    return np.tile(idx.reshape(-1, 16).T, (8, 1)).astype(np.uint16)


def unstriped(offs):
    return offs[:16].T.reshape(-1).astype(np.int64)


def sigmoid(v):
    return 1.0 / (1.0 + np.exp(-np.maximum(v, -700.0)))


def gelu(v):
    return 0.5 * v * (1.0 + np.tanh(np.sqrt(2.0 / np.pi) * (v + 0.044715 * v**3)))


K, T, S, N = 1024, 1024, 512, 256


def setup_inputs():
    n = np.random.standard_normal
    s = mx_kscale(K)[:, None]
    return {
        "xT": (n((K, T)) * s).astype(np.float32),
        "res": n((N, T)).astype(np.float32),
        "w1": (n((K, N)) / np.sqrt(K) / s).astype(np.float32),
        "w2": (n((K, N)) / np.sqrt(K) / s).astype(np.float32),
        "offs": striped(np.random.permutation(T)[:S]),
    }


def reference(xT, res, w1, w2, offs):
    r = f64(res)[:, unstriped(offs)]
    xq = mxq(f64(xT)[:, unstriped(offs)], 0, "e4m3")
    g = sigmoid(mxq(f64(w2), 0, "e4m3").T @ xq)
    y = gelu(mxq(f64(w1), 0, "e4m3").T @ xq)
    return r + g * (y - r)

@@ -1,0 +1,192 @@
+from contextlib import ExitStack
+
+import concourse.mybir as mybir
+
+K, T, S, N = 1024, 1024, 512, 256
+FLOPS = 2 * 2 * K * S * N
+
+F32 = mybir.dt.float32
+BF16 = mybir.dt.bfloat16
+U32 = mybir.dt.uint32
+I32 = mybir.dt.int32
+U16 = mybir.dt.uint16
+U8 = mybir.dt.uint8
+FP8X4 = mybir.dt.float8_e4m3fn_x4
+ACT = mybir.ActivationFunctionType
+ALU = mybir.AluOpType
+
+P = 128
+PACK = 4
+K_PASS = P * PACK
+PASSES = K // K_PASS
+BLOCKS = N // P
+HALF = S // 2
+VEC_COLS = [640,640,640,640]
+
+
+def tile_picked_highway_gelu_l_kernel(tc, xT, res, w1, w2, offs, out):
+    nc = tc.nc
+    with ExitStack() as ctx:
+        keep = ctx.enter_context(tc.tile_pool(name="keep", bufs=1))
+        psum = ctx.enter_context(tc.psum_pool(name="psum", bufs=1))
+
+        def sb(name, shape, dtype, on=None):
+            return keep.tile(shape, dtype, name=name, tag=on or name, align_bytes=64)
+
+        offsets = keep.tile([P, S // 16], U16, name="offsets")
+        warm_in = sb("warm_in", [P, 1], F32)
+        warm_out = sb("warm_out", [P, 1], F32)
+        nc.vector.memset(warm_in[:], 0.0)
+        nc.scalar.activation(warm_out[:], warm_in[:], ACT.Gelu_apprx_tanh)
+
+        halves = [slice(h * HALF, (h + 1) * HALF) for h in range(2)]
+        blocks = [slice(b * P, (b + 1) * P) for b in range(BLOCKS)]
+        everything = slice(0, N)
+
+        x_raw = []
+        for q in range(2 * PASSES):
+            g, u = divmod(q, 2)
+            t = sb(f"x_raw{q}", [P, 2, T], F32)
+            rows = xT[g * K_PASS : (g + 1) * K_PASS, :].rearrange("(p j) c -> p j c", j=PACK)
+            nc.sync.dma_start(t[:], rows[:, 2 * u : 2 * u + 2, :])
+            x_raw.append(t)
+            if q == 0:
+                nc.sync.dma_start(offsets[:], offs)
+
+        def load_w(w, name, g):
+            t = sb(name, [P, PACK, N], F32)
+            nc.sync.dma_start(t[:], w[g * K_PASS : (g + 1) * K_PASS, :].rearrange("(p j) m -> p j m", j=PACK))
+            return t
+
+        def load_res(b):
+            t = sb(f"res_raw{b}", [P, T], F32)
+            nc.sync.dma_start(t[:], res[blocks[b], :])
+            return t
+
+        w1a_raw = load_w(w1, "w1a_raw", 0)
+        w1b_raw = load_w(w1, "w1b_raw", 1)
+        w2a_raw = load_w(w2, "w2a_raw", 0)
+        res_raw = [load_res(b) for b in range(BLOCKS)]
+        w2b_raw = load_w(w2, "w2b_raw", 1)
+
+        picked = [sb(f"picked{g}", [P, 2, S], U32) for g in range(PASSES)]
+        woven = [sb(f"woven{g}", [P, S * PACK], BF16) for g in range(PASSES)]
+        x_codes = [sb(f"x_codes{g}", [P, S], U32) for g in range(PASSES)]
+        x_scales = [sb(f"x_scales{g}", [P, S], U8) for g in range(PASSES)]
+
+        def pick_pair(q):
+            g, u = divmod(q, 2)
+            pairs = sb(f"pairs{q}", [P, T, 2], BF16)
+            src = x_raw[q][:].rearrange("p e c -> p c e")
+            v = VEC_COLS[q]
+            nc.scalar.copy(pairs[:, v:, :], src[:, v:, :])
+            nc.vector.tensor_copy(pairs[:, :v, :], src[:, :v, :])
+            words = pairs[:].rearrange("p c e -> p (c e)").bitcast(U32)
+            nc.vector.tensor_copy(picked[g][:, u, :], words.indirect(offsets[:]))
+
+        def weave(copy, dtype, g, toks):
+            dst = woven[g][:].bitcast(dtype).rearrange("p (s u) -> p s u", u=2)
+            src = picked[g][:].bitcast(dtype).rearrange("p u s -> p s u")
+            copy(dst[:, toks, :], src[:, toks, :])
+
+        def quant_x(g, toks):
+            nc.vector.quantize_mx(
+                out=x_codes[g][:, toks].bitcast(FP8X4),
+                scales=x_scales[g][:, toks],
+                in_=woven[g][:, toks.start * PACK : toks.stop * PACK],
+            )
+
+        def round_w(copy, wq, raw, cols):
+            copy(
+                wq[0][:, cols, :].rearrange("p (c i) j -> p c j i", i=4),
+                raw[:, :, cols].rearrange("p j (c i) -> p c j i", i=4),
+            )
+
+        def quant_w(wq, cols):
+            nc.vector.quantize_mx(
+                out=wq[1][:, cols].bitcast(FP8X4),
+                scales=wq[2][:, cols],
+                in_=wq[0][:, cols, :].rearrange("p m j -> p (m j)"),
+            )
+
+        def w_tiles(name, on):
+            return (
+                sb(name + "_grouped", [P, N, PACK], BF16, on=on),
+                sb(name + "_codes", [P, N], U32),
+                sb(name + "_scales", [P, N], U8),
+            )
+
+        def mm(bank, wq, g, b, toks):
+            nc.tensor.matmul_mx(
+                out=bank,
+                lhsT=wq[1][:, blocks[b]].bitcast(FP8X4),
+                lhsT_scale=wq[2][:, blocks[b]],
+                rhs=x_codes[g][:, toks].bitcast(FP8X4),
+                rhs_scale=x_scales[g][:, toks],
+                start=(g == 0),
+                stop=(g == PASSES - 1),
+            )
+
+        y_bank = [psum.tile([P, S], F32, name=f"y_bank{b}") for b in range(BLOCKS)]
+        g_bank = [[psum.tile([P, HALF], F32, name=f"g_bank{b}{h}") for h in range(2)] for b in range(BLOCKS)]
+        all_toks = slice(0, S)
+
+        pick_pair(0)
+        pick_pair(1)
+        pick_pair(2)
+        weave(nc.scalar.copy, U32, 0, all_toks)
+        quant_x(0, all_toks)
+        pick_pair(3)
+        for toks in halves:
+            weave(nc.vector.tensor_copy, I32, 1, toks)
+        w1a = w_tiles("w1a", "x_raw3")
+        round_w(nc.scalar.copy, w1a, w1a_raw, everything)
+        quant_w(w1a, everything)
+        for b in range(BLOCKS):
+            mm(y_bank[b][:], w1a, 0, b, all_toks)
+        for toks in halves:
+            quant_x(1, toks)
+        w1b = w_tiles("w1b", "w1a_raw")
+        round_w(nc.scalar.copy, w1b, w1b_raw, everything)
+        quant_w(w1b, everything)
+        for b in range(BLOCKS):
+            mm(y_bank[b][:], w1b, 1, b, all_toks)
+        w2a = w_tiles("w2a", "w1b_raw")
+        round_w(nc.scalar.copy, w2a, w2a_raw, everything)
+
+        r = [sb("r0", [P, S], F32, on="w1a_raw"), None]
+        nc.vector.tensor_copy(r[0][:], res_raw[0][:].indirect(offsets[:]))
+        quant_w(w2a, everything)
+        for b in range(BLOCKS):
+            for h in range(2):
+                mm(g_bank[b][h][:], w2a, 0, b, halves[h])
+        r[1] = sb("r1", [P, S], F32, on="w1b_raw")
+        nc.vector.tensor_copy(r[1][:], res_raw[1][:].indirect(offsets[:]))
+
+        y = [sb(f"y{b}", [P, S], F32) for b in range(BLOCKS)]
+        for b in range(BLOCKS):
+            nc.scalar.activation(y[b][:], y_bank[b][:], ACT.Gelu_apprx_tanh)
+        d = [sb("d0", [P, S], F32), None]
+        nc.vector.tensor_tensor(d[0][:], y[0][:], r[0][:], ALU.subtract)
+
+        w2b = w_tiles("w2b", "w1b_codes")
+        for b in range(BLOCKS):
+            round_w(nc.scalar.copy, w2b, w2b_raw, blocks[b])
+        for b in range(BLOCKS):
+            quant_w(w2b, blocks[b])
+            for h in range(2):
+                mm(g_bank[b][h][:], w2b, 1, b, halves[h])
+        d[1] = sb("d1", [P, S], F32, on="w1b_codes")
+        nc.vector.tensor_tensor(d[1][:], y[1][:], r[1][:], ALU.subtract)
+
+        for b in range(BLOCKS):
+            th = sb(f"tanh{b}", [P, S], F32)
+            e = sb(f"e{b}", [P, S], F32)
+            o = sb(f"o{b}", [P, S], F32)
+            for h in range(2):
+                nc.scalar.activation(th[:, halves[h]], g_bank[b][h][:], ACT.Tanh, scale=0.5)
+            for h in range(2):
+                nc.vector.scalar_tensor_tensor(e[:, halves[h]], th[:, halves[h]], 1.0, d[b][:, halves[h]], ALU.add, ALU.mult)
+            for h in range(2):
+                nc.vector.scalar_tensor_tensor(o[:, halves[h]], e[:, halves[h]], 0.5, r[b][:, halves[h]], ALU.mult, ALU.add)
+                nc.sync.dma_start(out[blocks[b], halves[h]], o[:, halves[h]])

@@ -21,7 +21,7 @@ K_PASS = P * PACK
 PASSES = K // K_PASS
 BLOCKS = N // P
 HALF = S // 2
-VEC_COLS = [640,640,640,640]
+VEC_COLS = [640,640,576,352]
 
 
 def tile_picked_highway_gelu_l_kernel(tc, xT, res, w1, w2, offs, out):
@@ -64,25 +64,28 @@ def tile_picked_highway_gelu_l_kernel(tc, xT, res, w1, w2, offs, out):
             return t
 
         w1a_raw = load_w(w1, "w1a_raw", 0)
+        res_raw = [load_res(0), None]
         w1b_raw = load_w(w1, "w1b_raw", 1)
         w2a_raw = load_w(w2, "w2a_raw", 0)
-        res_raw = [load_res(b) for b in range(BLOCKS)]
         w2b_raw = load_w(w2, "w2b_raw", 1)
+        res_raw[1] = load_res(1)
 
         picked = [sb(f"picked{g}", [P, 2, S], U32) for g in range(PASSES)]
-        woven = [sb(f"woven{g}", [P, S * PACK], BF16) for g in range(PASSES)]
+        woven = [None, None]
         x_codes = [sb(f"x_codes{g}", [P, S], U32) for g in range(PASSES)]
         x_scales = [sb(f"x_scales{g}", [P, S], U8) for g in range(PASSES)]
 
-        def pick_pair(q):
-            g, u = divmod(q, 2)
+        def round_pair(q):
             pairs = sb(f"pairs{q}", [P, T, 2], BF16)
             src = x_raw[q][:].rearrange("p e c -> p c e")
             v = VEC_COLS[q]
             nc.scalar.copy(pairs[:, v:, :], src[:, v:, :])
             nc.vector.tensor_copy(pairs[:, :v, :], src[:, :v, :])
-            words = pairs[:].rearrange("p c e -> p (c e)").bitcast(U32)
-            nc.vector.tensor_copy(picked[g][:, u, :], words.indirect(offsets[:]))
+            return pairs[:].rearrange("p c e -> p (c e)").bitcast(U32)
+
+        def gather_pair(q, words, toks):
+            g, u = divmod(q, 2)
+            nc.vector.tensor_copy(picked[g][:, u, toks], words.indirect(offsets[:, toks.start // 16 : toks.stop // 16]))
 
         def weave(copy, dtype, g, toks):
             dst = woven[g][:].bitcast(dtype).rearrange("p (s u) -> p s u", u=2)
@@ -109,9 +112,9 @@ def tile_picked_highway_gelu_l_kernel(tc, xT, res, w1, w2, offs, out):
                 in_=wq[0][:, cols, :].rearrange("p m j -> p (m j)"),
             )
 
-        def w_tiles(name, on):
+        def w_tiles(name):
             return (
-                sb(name + "_grouped", [P, N, PACK], BF16, on=on),
+                sb(name + "_grouped", [P, N, PACK], BF16),
                 sb(name + "_codes", [P, N], U32),
                 sb(name + "_scales", [P, N], U8),
             )
@@ -131,53 +134,55 @@ def tile_picked_highway_gelu_l_kernel(tc, xT, res, w1, w2, offs, out):
         g_bank = [[psum.tile([P, HALF], F32, name=f"g_bank{b}{h}") for h in range(2)] for b in range(BLOCKS)]
         all_toks = slice(0, S)
 
-        pick_pair(0)
-        pick_pair(1)
-        pick_pair(2)
+        for q in range(3):
+            gather_pair(q, round_pair(q), all_toks)
+        woven[0] = sb("woven0", [P, S * PACK], BF16, on="x_raw2")
         weave(nc.scalar.copy, U32, 0, all_toks)
+        last_words = round_pair(3)
         quant_x(0, all_toks)
-        pick_pair(3)
         for toks in halves:
-            weave(nc.vector.tensor_copy, I32, 1, toks)
-        w1a = w_tiles("w1a", "x_raw3")
+            gather_pair(3, last_words, toks)
+        w1a = w_tiles("w1a")
         round_w(nc.scalar.copy, w1a, w1a_raw, everything)
         quant_w(w1a, everything)
         for b in range(BLOCKS):
             mm(y_bank[b][:], w1a, 0, b, all_toks)
+        woven[1] = sb("woven1", [P, S * PACK], BF16, on="w1a_raw")
+        weave(nc.scalar.copy, U32, 1, halves[0])
+        weave(nc.vector.tensor_copy, I32, 1, halves[1])
         for toks in halves:
             quant_x(1, toks)
-        w1b = w_tiles("w1b", "w1a_raw")
+        w1b = w_tiles("w1b")
         round_w(nc.scalar.copy, w1b, w1b_raw, everything)
         quant_w(w1b, everything)
         for b in range(BLOCKS):
             mm(y_bank[b][:], w1b, 1, b, all_toks)
-        w2a = w_tiles("w2a", "w1b_raw")
+        w2a = w_tiles("w2a")
         round_w(nc.scalar.copy, w2a, w2a_raw, everything)
 
-        r = [sb("r0", [P, S], F32, on="w1a_raw"), None]
-        nc.vector.tensor_copy(r[0][:], res_raw[0][:].indirect(offsets[:]))
+        r_both = sb("r", [P, BLOCKS * S], F32)
+        r = [r_both[:, b * S : (b + 1) * S] for b in range(BLOCKS)]
+        nc.vector.tensor_copy(r[0], res_raw[0][:].indirect(offsets[:]))
         quant_w(w2a, everything)
         for b in range(BLOCKS):
             for h in range(2):
                 mm(g_bank[b][h][:], w2a, 0, b, halves[h])
-        r[1] = sb("r1", [P, S], F32, on="w1b_raw")
-        nc.vector.tensor_copy(r[1][:], res_raw[1][:].indirect(offsets[:]))
-
-        y = [sb(f"y{b}", [P, S], F32) for b in range(BLOCKS)]
-        for b in range(BLOCKS):
-            nc.scalar.activation(y[b][:], y_bank[b][:], ACT.Gelu_apprx_tanh)
-        d = [sb("d0", [P, S], F32), None]
-        nc.vector.tensor_tensor(d[0][:], y[0][:], r[0][:], ALU.subtract)
-
-        w2b = w_tiles("w2b", "w1b_codes")
+        w2b = w_tiles("w2b")
         for b in range(BLOCKS):
             round_w(nc.scalar.copy, w2b, w2b_raw, blocks[b])
         for b in range(BLOCKS):
             quant_w(w2b, blocks[b])
             for h in range(2):
                 mm(g_bank[b][h][:], w2b, 1, b, halves[h])
-        d[1] = sb("d1", [P, S], F32, on="w1b_codes")
-        nc.vector.tensor_tensor(d[1][:], y[1][:], r[1][:], ALU.subtract)
+        y_both = sb("y", [P, BLOCKS * S], F32, on="w2b_raw")
+        y = [y_both[:, b * S : (b + 1) * S] for b in range(BLOCKS)]
+        for b in range(BLOCKS):
+            nc.scalar.activation(y[b], y_bank[b][:], ACT.Gelu_apprx_tanh)
+        nc.vector.tensor_copy(r[1], res_raw[1][:].indirect(offsets[:]))
+        both = sb("d", [P, BLOCKS * S], F32)
+        d = [both[:, b * S : (b + 1) * S] for b in range(BLOCKS)]
+        for b in range(BLOCKS):
+            nc.vector.tensor_tensor(d[b], y[b], r[b], ALU.subtract)
 
         for b in range(BLOCKS):
             th = sb(f"tanh{b}", [P, S], F32)

@@ -130,7 +130,7 @@ def tile_picked_highway_gelu_l_kernel(tc, xT, res, w1, w2, offs, out):
                 stop=(g == PASSES - 1),
             )
 
-        y_bank = [psum.tile([P, S], F32, name=f"y_bank{b}") for b in range(BLOCKS)]
+        y_bank = [[psum.tile([P, HALF], F32, name=f"y_bank{b}{h}") for h in range(2)] for b in range(BLOCKS)]
         g_bank = [[psum.tile([P, HALF], F32, name=f"g_bank{b}{h}") for h in range(2)] for b in range(BLOCKS)]
         all_toks = slice(0, S)
 
@@ -142,47 +142,46 @@ def tile_picked_highway_gelu_l_kernel(tc, xT, res, w1, w2, offs, out):
         quant_x(0, all_toks)
         for toks in halves:
             gather_pair(3, last_words, toks)
+        quarters = [(b, h) for b in range(BLOCKS) for h in range(2)]
         w1a = w_tiles("w1a")
         round_w(nc.scalar.copy, w1a, w1a_raw, everything)
         quant_w(w1a, everything)
-        for b in range(BLOCKS):
-            mm(y_bank[b][:], w1a, 0, b, all_toks)
-        woven[1] = sb("woven1", [P, S * PACK], BF16, on="w1a_raw")
+        for b, h in quarters:
+            mm(y_bank[b][h][:], w1a, 0, b, halves[h])
+        late = sb("late", [P, 3 * S], F32, on="w1a_raw")
+        woven[1] = late[:, : 2 * S].bitcast(BF16)
         weave(nc.scalar.copy, U32, 1, halves[0])
-        weave(nc.vector.tensor_copy, I32, 1, halves[1])
-        for toks in halves:
-            quant_x(1, toks)
+        weave(nc.gpsimd.tensor_copy, U32, 1, halves[1])
+        r = [late[:, 2 * S :], sb("r1", [P, S], F32)]
+        nc.vector.tensor_copy(r[0][:], res_raw[0][:].indirect(offsets[:]))
         w1b = w_tiles("w1b")
         round_w(nc.scalar.copy, w1b, w1b_raw, everything)
+        quant_x(1, halves[0])
         quant_w(w1b, everything)
-        for b in range(BLOCKS):
-            mm(y_bank[b][:], w1b, 1, b, all_toks)
+        quant_x(1, halves[1])
+        for b, h in quarters:
+            mm(y_bank[b][h][:], w1b, 1, b, halves[h])
         w2a = w_tiles("w2a")
         round_w(nc.scalar.copy, w2a, w2a_raw, everything)
-
-        r_both = sb("r", [P, BLOCKS * S], F32)
-        r = [r_both[:, b * S : (b + 1) * S] for b in range(BLOCKS)]
-        nc.vector.tensor_copy(r[0], res_raw[0][:].indirect(offsets[:]))
-        quant_w(w2a, everything)
-        for b in range(BLOCKS):
-            for h in range(2):
-                mm(g_bank[b][h][:], w2a, 0, b, halves[h])
         w2b = w_tiles("w2b")
-        for b in range(BLOCKS):
-            round_w(nc.scalar.copy, w2b, w2b_raw, blocks[b])
-        for b in range(BLOCKS):
+        round_w(nc.scalar.copy, w2b, w2b_raw, blocks[0])
+        round_w(nc.vector.tensor_copy, w2b, w2b_raw, blocks[1])
+        quant_w(w2a, everything)
+        for b, h in quarters:
+            mm(g_bank[b][h][:], w2a, 0, b, halves[h])
+        for b in reversed(range(BLOCKS)):
             quant_w(w2b, blocks[b])
-            for h in range(2):
-                mm(g_bank[b][h][:], w2b, 1, b, halves[h])
+        for b, h in quarters:
+            mm(g_bank[b][h][:], w2b, 1, b, halves[h])
         y_both = sb("y", [P, BLOCKS * S], F32, on="w2b_raw")
         y = [y_both[:, b * S : (b + 1) * S] for b in range(BLOCKS)]
-        for b in range(BLOCKS):
-            nc.scalar.activation(y[b], y_bank[b][:], ACT.Gelu_apprx_tanh)
-        nc.vector.tensor_copy(r[1], res_raw[1][:].indirect(offsets[:]))
-        both = sb("d", [P, BLOCKS * S], F32)
-        d = [both[:, b * S : (b + 1) * S] for b in range(BLOCKS)]
-        for b in range(BLOCKS):
-            nc.vector.tensor_tensor(d[b], y[b], r[b], ALU.subtract)
+        for b, h in quarters:
+            nc.scalar.activation(y[b][:, halves[h]], y_bank[b][h][:], ACT.Gelu_apprx_tanh)
+        nc.vector.tensor_copy(r[1][:], res_raw[1][:].indirect(offsets[:]))
+        d = [sb(f"d{b}", [P, S], F32) for b in range(BLOCKS)]
+        nc.gpsimd.tensor_tensor(d[0][:, halves[0]], y[0][:, halves[0]], r[0][:, halves[0]], ALU.subtract)
+        nc.vector.tensor_tensor(d[0][:, halves[1]], y[0][:, halves[1]], r[0][:, halves[1]], ALU.subtract)
+        nc.vector.tensor_tensor(d[1][:], y[1], r[1][:], ALU.subtract)
 
         for b in range(BLOCKS):
             th = sb(f"tanh{b}", [P, S], F32)

@@ -28,15 +28,19 @@ def tile_picked_highway_gelu_l_kernel(tc, xT, res, w1, w2, offs, out):
     nc = tc.nc
     with ExitStack() as ctx:
         keep = ctx.enter_context(tc.tile_pool(name="keep", bufs=1))
+        shared = ctx.enter_context(tc.tile_pool(name="shared", bufs=1))
         psum = ctx.enter_context(tc.psum_pool(name="psum", bufs=1))
 
         def sb(name, shape, dtype, on=None):
             return keep.tile(shape, dtype, name=name, tag=on or name, align_bytes=64)
 
+        def placed(name, shape, offset):
+            return shared.tile(shape, F32, name=name, offset=offset, align_bytes=64)
+
         offsets = keep.tile([P, S // 16], U16, name="offsets")
         warm_in = sb("warm_in", [P, 1], F32)
         warm_out = sb("warm_out", [P, 1], F32)
-        nc.vector.memset(warm_in[:], 0.0)
+        nc.gpsimd.memset(warm_in[:], 0.0)
         nc.scalar.activation(warm_out[:], warm_in[:], ACT.Gelu_apprx_tanh)
 
         halves = [slice(h * HALF, (h + 1) * HALF) for h in range(2)]
@@ -54,7 +58,7 @@ def tile_picked_highway_gelu_l_kernel(tc, xT, res, w1, w2, offs, out):
                 nc.sync.dma_start(offsets[:], offs)
 
         def load_w(w, name, g):
-            t = sb(name, [P, PACK, N], F32)
+            t = placed(name, [P, PACK, N], 0) if name == "w2b_raw" else sb(name, [P, PACK, N], F32)
             nc.sync.dma_start(t[:], w[g * K_PASS : (g + 1) * K_PASS, :].rearrange("(p j) m -> p j m", j=PACK))
             return t
 
@@ -148,12 +152,12 @@ def tile_picked_highway_gelu_l_kernel(tc, xT, res, w1, w2, offs, out):
         quant_w(w1a, everything)
         for b, h in quarters:
             mm(y_bank[b][h][:], w1a, 0, b, halves[h])
-        late = sb("late", [P, 3 * S], F32, on="w1a_raw")
+        late = sb("late", [P, 4 * S], F32, on="w1a_raw")
         woven[1] = late[:, : 2 * S].bitcast(BF16)
         weave(nc.scalar.copy, U32, 1, halves[0])
         weave(nc.gpsimd.tensor_copy, U32, 1, halves[1])
-        r = [late[:, 2 * S :], sb("r1", [P, S], F32)]
-        nc.vector.tensor_copy(r[0][:], res_raw[0][:].indirect(offsets[:]))
+        r = late[:, 2 * S :]
+        nc.vector.tensor_copy(r[:, :S], res_raw[0][:].indirect(offsets[:]))
         w1b = w_tiles("w1b")
         round_w(nc.scalar.copy, w1b, w1b_raw, everything)
         quant_x(1, halves[0])
@@ -164,33 +168,44 @@ def tile_picked_highway_gelu_l_kernel(tc, xT, res, w1, w2, offs, out):
         w2a = w_tiles("w2a")
         round_w(nc.scalar.copy, w2a, w2a_raw, everything)
         w2b = w_tiles("w2b")
-        round_w(nc.scalar.copy, w2b, w2b_raw, blocks[0])
-        round_w(nc.vector.tensor_copy, w2b, w2b_raw, blocks[1])
+        round_w(nc.vector.tensor_copy, w2b, w2b_raw, blocks[0])
+        round_w(nc.scalar.copy, w2b, w2b_raw, blocks[1])
         quant_w(w2a, everything)
         for b, h in quarters:
             mm(g_bank[b][h][:], w2a, 0, b, halves[h])
-        for b in reversed(range(BLOCKS)):
+        for b in range(BLOCKS):
             quant_w(w2b, blocks[b])
         for b, h in quarters:
             mm(g_bank[b][h][:], w2b, 1, b, halves[h])
-        y_both = sb("y", [P, BLOCKS * S], F32, on="w2b_raw")
-        y = [y_both[:, b * S : (b + 1) * S] for b in range(BLOCKS)]
-        for b, h in quarters:
-            nc.scalar.activation(y[b][:, halves[h]], y_bank[b][h][:], ACT.Gelu_apprx_tanh)
-        nc.vector.tensor_copy(r[1][:], res_raw[1][:].indirect(offsets[:]))
-        d = [sb(f"d{b}", [P, S], F32) for b in range(BLOCKS)]
-        nc.gpsimd.tensor_tensor(d[0][:, halves[0]], y[0][:, halves[0]], r[0][:, halves[0]], ALU.subtract)
-        nc.vector.tensor_tensor(d[0][:, halves[1]], y[0][:, halves[1]], r[0][:, halves[1]], ALU.subtract)
-        nc.vector.tensor_tensor(d[1][:], y[1], r[1][:], ALU.subtract)
+        cols = [slice(i * HALF, (i + 1) * HALF) for i in range(4)]
+        y_first = placed("y_first", [P, HALF], 3 * HALF * 4)
+        y_rest = placed("y_rest", [P, 3 * HALF], 0)
+        for i, (b, h) in enumerate(quarters):
+            nc.scalar.activation(y_first[:] if i == 0 else y_rest[:, cols[i - 1]], y_bank[b][h][:], ACT.Gelu_apprx_tanh)
+        for h in range(2):
+            nc.vector.tensor_copy(r[:, cols[2 + h]], res_raw[1][:].indirect(offsets[:, h * HALF // 16 : (h + 1) * HALF // 16]))
+        d = sb("d", [P, BLOCKS * S], F32, on="w2a_grouped")
+        nc.gpsimd.tensor_tensor(d[:, cols[0]], y_first[:], r[:, cols[0]], ALU.subtract)
+        for c in (slice(HALF, 3 * HALF), cols[3]):
+            nc.vector.tensor_tensor(d[:, c], y_rest[:, c.start - HALF : c.stop - HALF], r[:, c], ALU.subtract)
+        th = sb("tanh", [P, BLOCKS * S], F32)
+        for i, (b, h) in enumerate(quarters):
+            nc.scalar.activation(th[:, cols[i]], g_bank[b][h][:], ACT.Tanh, scale=0.5)
+        e = placed("e", [P, BLOCKS * S], 3 * HALF * 4)
+        o = sb("o", [P, BLOCKS * S], F32)
 
-        for b in range(BLOCKS):
-            th = sb(f"tanh{b}", [P, S], F32)
-            e = sb(f"e{b}", [P, S], F32)
-            o = sb(f"o{b}", [P, S], F32)
-            for h in range(2):
-                nc.scalar.activation(th[:, halves[h]], g_bank[b][h][:], ACT.Tanh, scale=0.5)
-            for h in range(2):
-                nc.vector.scalar_tensor_tensor(e[:, halves[h]], th[:, halves[h]], 1.0, d[b][:, halves[h]], ALU.add, ALU.mult)
-            for h in range(2):
-                nc.vector.scalar_tensor_tensor(o[:, halves[h]], e[:, halves[h]], 0.5, r[b][:, halves[h]], ALU.mult, ALU.add)
-                nc.sync.dma_start(out[blocks[b], halves[h]], o[:, halves[h]])
+        def gate(c):
+            nc.vector.scalar_tensor_tensor(e[:, c], th[:, c], 1.0, d[:, c], ALU.add, ALU.mult)
+
+        def finish(i):
+            b, h = quarters[i]
+            nc.vector.scalar_tensor_tensor(o[:, cols[i]], e[:, cols[i]], 0.5, r[:, cols[i]], ALU.mult, ALU.add)
+            nc.sync.dma_start(out[blocks[b], halves[h]], o[:, cols[i]])
+
+        gate(slice(0, S))
+        gate(cols[2])
+        finish(0)
+        finish(1)
+        gate(cols[3])
+        finish(2)
+        finish(3)

@@ -21,7 +21,7 @@ K_PASS = P * PACK
 PASSES = K // K_PASS
 BLOCKS = N // P
 HALF = S // 2
-VEC_COLS = [640,640,576,352]
+VEC_COLS = {0: 640, 1: 640, 3: T}
 
 
 def tile_picked_highway_gelu_l_kernel(tc, xT, res, w1, w2, offs, out):
@@ -50,9 +50,14 @@ def tile_picked_highway_gelu_l_kernel(tc, xT, res, w1, w2, offs, out):
         x_raw = []
         for q in range(2 * PASSES):
             g, u = divmod(q, 2)
-            t = sb(f"x_raw{q}", [P, 2, T], F32)
             rows = xT[g * K_PASS : (g + 1) * K_PASS, :].rearrange("(p j) c -> p j c", j=PACK)
-            nc.sync.dma_start(t[:], rows[:, 2 * u : 2 * u + 2, :])
+            if q == 2:
+                t = [sb(f"x_plane{j}", [P, T], F32) for j in range(2)]
+                for j in range(2):
+                    nc.sync.dma_start(t[j][:], rows[:, j, :])
+            else:
+                t = sb(f"x_raw{q}", [P, 2, T], F32)
+                nc.sync.dma_start(t[:], rows[:, 2 * u : 2 * u + 2, :])
             x_raw.append(t)
             if q == 0:
                 nc.sync.dma_start(offsets[:], offs)
@@ -74,7 +79,7 @@ def tile_picked_highway_gelu_l_kernel(tc, xT, res, w1, w2, offs, out):
         w2b_raw = load_w(w2, "w2b_raw", 1)
         res_raw[1] = load_res(1)
 
-        picked = [sb(f"picked{g}", [P, 2, S], U32) for g in range(PASSES)]
+        picked = [sb("picked0", [P, 2, S], U32)]
         woven = [None, None]
         x_codes = [sb(f"x_codes{g}", [P, S], U32) for g in range(PASSES)]
         x_scales = [sb(f"x_scales{g}", [P, S], U8) for g in range(PASSES)]
@@ -83,7 +88,8 @@ def tile_picked_highway_gelu_l_kernel(tc, xT, res, w1, w2, offs, out):
             pairs = sb(f"pairs{q}", [P, T, 2], BF16)
             src = x_raw[q][:].rearrange("p e c -> p c e")
             v = VEC_COLS[q]
-            nc.scalar.copy(pairs[:, v:, :], src[:, v:, :])
+            if v < T:
+                nc.scalar.copy(pairs[:, v:, :], src[:, v:, :])
             nc.vector.tensor_copy(pairs[:, :v, :], src[:, :v, :])
             return pairs[:].rearrange("p c e -> p (c e)").bitcast(U32)
 
@@ -138,25 +144,34 @@ def tile_picked_highway_gelu_l_kernel(tc, xT, res, w1, w2, offs, out):
         g_bank = [[psum.tile([P, HALF], F32, name=f"g_bank{b}{h}") for h in range(2)] for b in range(BLOCKS)]
         all_toks = slice(0, S)
 
-        for q in range(3):
-            gather_pair(q, round_pair(q), all_toks)
-        woven[0] = sb("woven0", [P, S * PACK], BF16, on="x_raw2")
-        weave(nc.scalar.copy, U32, 0, all_toks)
-        last_words = round_pair(3)
-        quant_x(0, all_toks)
+        gather_pair(0, round_pair(0), all_toks)
+        words = round_pair(1)
         for toks in halves:
-            gather_pair(3, last_words, toks)
+            gather_pair(1, words, toks)
+        planes = [sb(f"plane{j}", [P, T], BF16) for j in range(2)]
+        nc.scalar.copy(planes[0][:], x_raw[2][0][:])
+        for c in (slice(0, T // 2), slice(T // 2, T)):
+            nc.vector.tensor_copy(planes[1][:, c], x_raw[2][1][:, c])
+        woven[1] = sb("woven1", [P, S * PACK], BF16)
+        by_slot = woven[1][:].rearrange("p (s t) -> p t s", t=PACK)
+        for j in range(2):
+            nc.scalar.activation(by_slot[:, j, :], planes[j][:].indirect(offsets[:]), ACT.Copy)
+        woven[0] = x_raw[2][1][:].bitcast(BF16)
+        for toks in halves:
+            weave(nc.vector.tensor_copy, I32, 0, toks)
+        for toks in halves:
+            quant_x(0, toks)
+        last_words = round_pair(3)
+        by_word = woven[1][:].bitcast(U32).rearrange("p (s u) -> p u s", u=2)
+        for toks in halves:
+            nc.vector.tensor_copy(by_word[:, 1, toks], last_words.indirect(offsets[:, toks.start // 16 : toks.stop // 16]))
         quarters = [(b, h) for b in range(BLOCKS) for h in range(2)]
         w1a = w_tiles("w1a")
         round_w(nc.scalar.copy, w1a, w1a_raw, everything)
         quant_w(w1a, everything)
         for b, h in quarters:
             mm(y_bank[b][h][:], w1a, 0, b, halves[h])
-        late = sb("late", [P, 4 * S], F32, on="w1a_raw")
-        woven[1] = late[:, : 2 * S].bitcast(BF16)
-        weave(nc.scalar.copy, U32, 1, halves[0])
-        weave(nc.gpsimd.tensor_copy, U32, 1, halves[1])
-        r = late[:, 2 * S :]
+        r = sb("r", [P, 2 * S], F32, on="w1a_raw")
         nc.vector.tensor_copy(r[:, :S], res_raw[0][:].indirect(offsets[:]))
         w1b = w_tiles("w1b")
         round_w(nc.scalar.copy, w1b, w1b_raw, everything)
@@ -184,7 +199,7 @@ def tile_picked_highway_gelu_l_kernel(tc, xT, res, w1, w2, offs, out):
             nc.scalar.activation(y_first[:] if i == 0 else y_rest[:, cols[i - 1]], y_bank[b][h][:], ACT.Gelu_apprx_tanh)
         for h in range(2):
             nc.vector.tensor_copy(r[:, cols[2 + h]], res_raw[1][:].indirect(offsets[:, h * HALF // 16 : (h + 1) * HALF // 16]))
-        d = sb("d", [P, BLOCKS * S], F32, on="w2a_grouped")
+        d = sb("d", [P, BLOCKS * S], F32, on="w2b_grouped")
         nc.gpsimd.tensor_tensor(d[:, cols[0]], y_first[:], r[:, cols[0]], ALU.subtract)
         for c in (slice(HALF, 3 * HALF), cols[3]):
             nc.vector.tensor_tensor(d[:, c], y_rest[:, c.start - HALF : c.stop - HALF], r[:, c], ALU.subtract)

@@ -72,8 +72,8 @@ def tile_picked_highway_gelu_l_kernel(tc, xT, res, w1, w2, offs, out):
             nc.sync.dma_start(t[:], res[blocks[b], :])
             return t
 
-        w1a_raw = load_w(w1, "w1a_raw", 0)
         res_raw = [load_res(0), None]
+        w1a_raw = load_w(w1, "w1a_raw", 0)
         w1b_raw = load_w(w1, "w1b_raw", 1)
         w2a_raw = load_w(w2, "w2a_raw", 0)
         w2b_raw = load_w(w2, "w2b_raw", 1)
@@ -162,6 +162,8 @@ def tile_picked_highway_gelu_l_kernel(tc, xT, res, w1, w2, offs, out):
         for toks in halves:
             quant_x(0, toks)
         last_words = round_pair(3)
+        r_first = sb("r_first", [P, HALF], F32)
+        nc.vector.tensor_copy(r_first[:], res_raw[0][:].indirect(offsets[:, : HALF // 16]))
         by_word = woven[1][:].bitcast(U32).rearrange("p (s u) -> p u s", u=2)
         for toks in halves:
             nc.vector.tensor_copy(by_word[:, 1, toks], last_words.indirect(offsets[:, toks.start // 16 : toks.stop // 16]))
@@ -171,8 +173,8 @@ def tile_picked_highway_gelu_l_kernel(tc, xT, res, w1, w2, offs, out):
         quant_w(w1a, everything)
         for b, h in quarters:
             mm(y_bank[b][h][:], w1a, 0, b, halves[h])
-        r = sb("r", [P, 2 * S], F32, on="w1a_raw")
-        nc.vector.tensor_copy(r[:, :S], res_raw[0][:].indirect(offsets[:]))
+        r = sb("r_rest", [P, 2 * S], F32, on="w1a_raw")
+        nc.vector.tensor_copy(r[:, HALF:S], res_raw[0][:].indirect(offsets[:, HALF // 16 :]))
         w1b = w_tiles("w1b")
         round_w(nc.scalar.copy, w1b, w1b_raw, everything)
         quant_x(1, halves[0])
@@ -200,7 +202,7 @@ def tile_picked_highway_gelu_l_kernel(tc, xT, res, w1, w2, offs, out):
         for h in range(2):
             nc.vector.tensor_copy(r[:, cols[2 + h]], res_raw[1][:].indirect(offsets[:, h * HALF // 16 : (h + 1) * HALF // 16]))
         d = sb("d", [P, BLOCKS * S], F32, on="w2b_grouped")
-        nc.gpsimd.tensor_tensor(d[:, cols[0]], y_first[:], r[:, cols[0]], ALU.subtract)
+        nc.gpsimd.tensor_tensor(d[:, cols[0]], y_first[:], r_first[:], ALU.subtract)
         for c in (slice(HALF, 3 * HALF), cols[3]):
             nc.vector.tensor_tensor(d[:, c], y_rest[:, c.start - HALF : c.stop - HALF], r[:, c], ALU.subtract)
         th = sb("tanh", [P, BLOCKS * S], F32)
@@ -214,7 +216,7 @@ def tile_picked_highway_gelu_l_kernel(tc, xT, res, w1, w2, offs, out):
 
         def finish(i):
             b, h = quarters[i]
-            nc.vector.scalar_tensor_tensor(o[:, cols[i]], e[:, cols[i]], 0.5, r[:, cols[i]], ALU.mult, ALU.add)
+            nc.vector.scalar_tensor_tensor(o[:, cols[i]], e[:, cols[i]], 0.5, r[:, cols[i]] if i else r_first[:], ALU.mult, ALU.add)
             nc.sync.dma_start(out[blocks[b], halves[h]], o[:, cols[i]])
 
         gate(slice(0, S))

@@ -21,7 +21,9 @@ K_PASS = P * PACK
 PASSES = K // K_PASS
 BLOCKS = N // P
 HALF = S // 2
-VEC_COLS = {0: 640, 1: 640, 3: T}
+GROUP = 16
+F32_BYTES = 4
+VECTOR_COLUMNS = 640
 
 
 def tile_picked_highway_gelu_l_kernel(tc, xT, res, w1, w2, offs, out):
@@ -34,92 +36,69 @@ def tile_picked_highway_gelu_l_kernel(tc, xT, res, w1, w2, offs, out):
         def sb(name, shape, dtype, on=None):
             return keep.tile(shape, dtype, name=name, tag=on or name, align_bytes=64)
 
-        def placed(name, shape, offset):
-            return shared.tile(shape, F32, name=name, offset=offset, align_bytes=64)
+        def placed(name, shape, column):
+            return shared.tile(shape, F32, name=name, offset=column * F32_BYTES, align_bytes=64)
 
-        offsets = keep.tile([P, S // 16], U16, name="offsets")
+        offsets = keep.tile([P, S // GROUP], U16, name="offsets")
         warm_in = sb("warm_in", [P, 1], F32)
         warm_out = sb("warm_out", [P, 1], F32)
-        nc.gpsimd.memset(warm_in[:], 0.0)
+        nc.vector.memset(warm_in[:], 0.0)
         nc.scalar.activation(warm_out[:], warm_in[:], ACT.Gelu_apprx_tanh)
 
+        all_toks = slice(0, S)
         halves = [slice(h * HALF, (h + 1) * HALF) for h in range(2)]
+        all_rows = slice(0, N)
         blocks = [slice(b * P, (b + 1) * P) for b in range(BLOCKS)]
-        everything = slice(0, N)
+        quarters = [(b, h) for b in range(BLOCKS) for h in range(2)]
+        cols = [slice(i * HALF, (i + 1) * HALF) for i in range(len(quarters))]
 
-        x_raw = []
-        for q in range(2 * PASSES):
-            g, u = divmod(q, 2)
-            rows = xT[g * K_PASS : (g + 1) * K_PASS, :].rearrange("(p j) c -> p j c", j=PACK)
-            if q == 2:
-                t = [sb(f"x_plane{j}", [P, T], F32) for j in range(2)]
-                for j in range(2):
-                    nc.sync.dma_start(t[j][:], rows[:, j, :])
-            else:
-                t = sb(f"x_raw{q}", [P, 2, T], F32)
-                nc.sync.dma_start(t[:], rows[:, 2 * u : 2 * u + 2, :])
-            x_raw.append(t)
-            if q == 0:
-                nc.sync.dma_start(offsets[:], offs)
+        def entries(toks):
+            return offsets[:, toks.start // GROUP : toks.stop // GROUP]
 
-        def load_w(w, name, g):
-            t = placed(name, [P, PACK, N], 0) if name == "w2b_raw" else sb(name, [P, PACK, N], F32)
-            nc.sync.dma_start(t[:], w[g * K_PASS : (g + 1) * K_PASS, :].rearrange("(p j) m -> p j m", j=PACK))
-            return t
+        def pass_rows(src, g):
+            return src[g * K_PASS : (g + 1) * K_PASS, :].rearrange("(p t) c -> p t c", t=PACK)
+
+        def load(tile, src):
+            nc.sync.dma_start(tile[:], src)
+            return tile
+
+        def load_pair(name, g, t):
+            return load(sb(name, [P, 2, T], F32), pass_rows(xT, g)[:, t : t + 2, :])
 
         def load_res(b):
-            t = sb(f"res_raw{b}", [P, T], F32)
-            nc.sync.dma_start(t[:], res[blocks[b], :])
-            return t
+            return load(sb(f"res_raw{b}", [P, T], F32), res[blocks[b], :])
 
-        res_raw = [load_res(0), None]
-        w1a_raw = load_w(w1, "w1a_raw", 0)
-        w1b_raw = load_w(w1, "w1b_raw", 1)
-        w2a_raw = load_w(w2, "w2a_raw", 0)
-        w2b_raw = load_w(w2, "w2b_raw", 1)
-        res_raw[1] = load_res(1)
+        x_pair0 = load_pair("x_raw0", 0, 0)
+        nc.sync.dma_start(offsets[:], offs)
+        x_pair1 = load_pair("x_raw1", 0, 2)
+        x_rows = [load(sb(f"x_plane{t}", [P, T], F32), pass_rows(xT, 1)[:, t, :]) for t in range(2)]
+        x_last = load_pair("x_raw3", 1, 2)
+        res0_raw = load_res(0)
+        w1a_raw = load(sb("w1a_raw", [P, PACK, N], F32), pass_rows(w1, 0))
+        w1b_raw = load(sb("w1b_raw", [P, PACK, N], F32), pass_rows(w1, 1))
+        w2a_raw = load(sb("w2a_raw", [P, PACK, N], F32), pass_rows(w2, 0))
+        w2b_raw = load(placed("w2b_raw", [P, PACK, N], 0), pass_rows(w2, 1))
+        res1_raw = load_res(1)
 
-        picked = [sb("picked0", [P, 2, S], U32)]
-        woven = [None, None]
+        picked = sb("picked0", [P, 2, S], U32)
         x_codes = [sb(f"x_codes{g}", [P, S], U32) for g in range(PASSES)]
         x_scales = [sb(f"x_scales{g}", [P, S], U8) for g in range(PASSES)]
 
-        def round_pair(q):
-            pairs = sb(f"pairs{q}", [P, T, 2], BF16)
-            src = x_raw[q][:].rearrange("p e c -> p c e")
-            v = VEC_COLS[q]
-            if v < T:
-                nc.scalar.copy(pairs[:, v:, :], src[:, v:, :])
-            nc.vector.tensor_copy(pairs[:, :v, :], src[:, :v, :])
-            return pairs[:].rearrange("p c e -> p (c e)").bitcast(U32)
+        def pair_views(name, raw):
+            pairs = sb(name, [P, T, 2], BF16)
+            return pairs, raw[:].rearrange("p e c -> p c e"), pairs[:].rearrange("p c e -> p (c e)").bitcast(U32)
 
-        def gather_pair(q, words, toks):
-            g, u = divmod(q, 2)
-            nc.vector.tensor_copy(picked[g][:, u, toks], words.indirect(offsets[:, toks.start // 16 : toks.stop // 16]))
+        def round_pair_shared(name, raw):
+            pairs, src, words = pair_views(name, raw)
+            nc.scalar.copy(pairs[:, VECTOR_COLUMNS:, :], src[:, VECTOR_COLUMNS:, :])
+            nc.vector.tensor_copy(pairs[:, :VECTOR_COLUMNS, :], src[:, :VECTOR_COLUMNS, :])
+            return words
 
-        def weave(copy, dtype, g, toks):
-            dst = woven[g][:].bitcast(dtype).rearrange("p (s u) -> p s u", u=2)
-            src = picked[g][:].bitcast(dtype).rearrange("p u s -> p s u")
-            copy(dst[:, toks, :], src[:, toks, :])
-
-        def quant_x(g, toks):
+        def quant_x(g, woven, toks):
             nc.vector.quantize_mx(
                 out=x_codes[g][:, toks].bitcast(FP8X4),
                 scales=x_scales[g][:, toks],
-                in_=woven[g][:, toks.start * PACK : toks.stop * PACK],
-            )
-
-        def round_w(copy, wq, raw, cols):
-            copy(
-                wq[0][:, cols, :].rearrange("p (c i) j -> p c j i", i=4),
-                raw[:, :, cols].rearrange("p j (c i) -> p c j i", i=4),
-            )
-
-        def quant_w(wq, cols):
-            nc.vector.quantize_mx(
-                out=wq[1][:, cols].bitcast(FP8X4),
-                scales=wq[2][:, cols],
-                in_=wq[0][:, cols, :].rearrange("p m j -> p (m j)"),
+                in_=woven[:, toks.start * PACK : toks.stop * PACK],
             )
 
         def w_tiles(name):
@@ -129,86 +108,107 @@ def tile_picked_highway_gelu_l_kernel(tc, xT, res, w1, w2, offs, out):
                 sb(name + "_scales", [P, N], U8),
             )
 
-        def mm(bank, wq, g, b, toks):
-            nc.tensor.matmul_mx(
-                out=bank,
-                lhsT=wq[1][:, blocks[b]].bitcast(FP8X4),
-                lhsT_scale=wq[2][:, blocks[b]],
-                rhs=x_codes[g][:, toks].bitcast(FP8X4),
-                rhs_scale=x_scales[g][:, toks],
-                start=(g == 0),
-                stop=(g == PASSES - 1),
+        def round_w(copy, tiles, raw, rows):
+            copy(
+                tiles[0][:, rows, :].rearrange("p (c i) t -> p c t i", i=4),
+                raw[:, :, rows].rearrange("p t (c i) -> p c t i", i=4),
             )
+
+        def quant_w(tiles, rows):
+            nc.vector.quantize_mx(
+                out=tiles[1][:, rows].bitcast(FP8X4),
+                scales=tiles[2][:, rows],
+                in_=tiles[0][:, rows, :].rearrange("p m t -> p (m t)"),
+            )
+
+        def multiply(banks, tiles, g):
+            for b, h in quarters:
+                nc.tensor.matmul_mx(
+                    out=banks[b][h][:],
+                    lhsT=tiles[1][:, blocks[b]].bitcast(FP8X4),
+                    lhsT_scale=tiles[2][:, blocks[b]],
+                    rhs=x_codes[g][:, halves[h]].bitcast(FP8X4),
+                    rhs_scale=x_scales[g][:, halves[h]],
+                    start=(g == 0),
+                    stop=(g == PASSES - 1),
+                )
 
         y_bank = [[psum.tile([P, HALF], F32, name=f"y_bank{b}{h}") for h in range(2)] for b in range(BLOCKS)]
         g_bank = [[psum.tile([P, HALF], F32, name=f"g_bank{b}{h}") for h in range(2)] for b in range(BLOCKS)]
-        all_toks = slice(0, S)
 
-        gather_pair(0, round_pair(0), all_toks)
-        words = round_pair(1)
+        words = round_pair_shared("pairs0", x_pair0)
+        nc.vector.tensor_copy(picked[:, 0, all_toks], words.indirect(entries(all_toks)))
+        words = round_pair_shared("pairs1", x_pair1)
         for toks in halves:
-            gather_pair(1, words, toks)
-        planes = [sb(f"plane{j}", [P, T], BF16) for j in range(2)]
-        nc.scalar.copy(planes[0][:], x_raw[2][0][:])
+            nc.vector.tensor_copy(picked[:, 1, toks], words.indirect(entries(toks)))
+
+        planes = [sb(f"plane{t}", [P, T], BF16) for t in range(2)]
+        nc.scalar.copy(planes[0][:], x_rows[0][:])
         for c in (slice(0, T // 2), slice(T // 2, T)):
-            nc.vector.tensor_copy(planes[1][:, c], x_raw[2][1][:, c])
-        woven[1] = sb("woven1", [P, S * PACK], BF16)
-        by_slot = woven[1][:].rearrange("p (s t) -> p t s", t=PACK)
-        for j in range(2):
-            nc.scalar.activation(by_slot[:, j, :], planes[j][:].indirect(offsets[:]), ACT.Copy)
-        woven[0] = x_raw[2][1][:].bitcast(BF16)
+            nc.vector.tensor_copy(planes[1][:, c], x_rows[1][:, c])
+        woven1 = sb("woven1", [P, S * PACK], BF16)
+        by_slot = woven1[:].rearrange("p (s t) -> p t s", t=PACK)
+        for t in range(2):
+            nc.scalar.activation(by_slot[:, t, :], planes[t][:].indirect(offsets[:]), ACT.Copy)
+
+        woven0 = x_rows[1][:].bitcast(BF16)
+        woven0_words = woven0.bitcast(I32).rearrange("p (s u) -> p s u", u=2)
+        picked_words = picked[:].bitcast(I32).rearrange("p u s -> p s u")
         for toks in halves:
-            weave(nc.vector.tensor_copy, I32, 0, toks)
+            nc.vector.tensor_copy(woven0_words[:, toks, :], picked_words[:, toks, :])
         for toks in halves:
-            quant_x(0, toks)
-        last_words = round_pair(3)
+            quant_x(0, woven0, toks)
+
+        pairs, src, words = pair_views("pairs3", x_last)
+        nc.vector.tensor_copy(pairs[:, :T, :], src[:, :T, :])
         r_first = sb("r_first", [P, HALF], F32)
-        nc.vector.tensor_copy(r_first[:], res_raw[0][:].indirect(offsets[:, : HALF // 16]))
-        by_word = woven[1][:].bitcast(U32).rearrange("p (s u) -> p u s", u=2)
+        nc.vector.tensor_copy(r_first[:], res0_raw[:].indirect(entries(halves[0])))
+        by_word = woven1[:].bitcast(U32).rearrange("p (s u) -> p u s", u=2)
         for toks in halves:
-            nc.vector.tensor_copy(by_word[:, 1, toks], last_words.indirect(offsets[:, toks.start // 16 : toks.stop // 16]))
-        quarters = [(b, h) for b in range(BLOCKS) for h in range(2)]
+            nc.vector.tensor_copy(by_word[:, 1, toks], words.indirect(entries(toks)))
+
         w1a = w_tiles("w1a")
-        round_w(nc.scalar.copy, w1a, w1a_raw, everything)
-        quant_w(w1a, everything)
-        for b, h in quarters:
-            mm(y_bank[b][h][:], w1a, 0, b, halves[h])
-        r = sb("r_rest", [P, 2 * S], F32, on="w1a_raw")
-        nc.vector.tensor_copy(r[:, HALF:S], res_raw[0][:].indirect(offsets[:, HALF // 16 :]))
+        round_w(nc.scalar.copy, w1a, w1a_raw, all_rows)
+        quant_w(w1a, all_rows)
+        multiply(y_bank, w1a, 0)
+        r_rest = sb("r_rest", [P, BLOCKS * S], F32, on="w1a_raw")
+        nc.vector.tensor_copy(r_rest[:, cols[1]], res0_raw[:].indirect(entries(halves[1])))
         w1b = w_tiles("w1b")
-        round_w(nc.scalar.copy, w1b, w1b_raw, everything)
-        quant_x(1, halves[0])
-        quant_w(w1b, everything)
-        quant_x(1, halves[1])
-        for b, h in quarters:
-            mm(y_bank[b][h][:], w1b, 1, b, halves[h])
+        round_w(nc.scalar.copy, w1b, w1b_raw, all_rows)
+        quant_x(1, woven1, halves[0])
+        quant_w(w1b, all_rows)
+        quant_x(1, woven1, halves[1])
+        multiply(y_bank, w1b, 1)
+
         w2a = w_tiles("w2a")
-        round_w(nc.scalar.copy, w2a, w2a_raw, everything)
+        round_w(nc.scalar.copy, w2a, w2a_raw, all_rows)
         w2b = w_tiles("w2b")
         round_w(nc.vector.tensor_copy, w2b, w2b_raw, blocks[0])
         round_w(nc.scalar.copy, w2b, w2b_raw, blocks[1])
-        quant_w(w2a, everything)
-        for b, h in quarters:
-            mm(g_bank[b][h][:], w2a, 0, b, halves[h])
+        quant_w(w2a, all_rows)
+        multiply(g_bank, w2a, 0)
         for b in range(BLOCKS):
             quant_w(w2b, blocks[b])
-        for b, h in quarters:
-            mm(g_bank[b][h][:], w2b, 1, b, halves[h])
-        cols = [slice(i * HALF, (i + 1) * HALF) for i in range(4)]
-        y_first = placed("y_first", [P, HALF], 3 * HALF * 4)
+        multiply(g_bank, w2b, 1)
+
+        y_first = placed("y_first", [P, HALF], 3 * HALF)
         y_rest = placed("y_rest", [P, 3 * HALF], 0)
+        y = [y_first[:]] + [y_rest[:, c] for c in cols[:3]]
         for i, (b, h) in enumerate(quarters):
-            nc.scalar.activation(y_first[:] if i == 0 else y_rest[:, cols[i - 1]], y_bank[b][h][:], ACT.Gelu_apprx_tanh)
+            nc.scalar.activation(y[i], y_bank[b][h][:], ACT.Gelu_apprx_tanh)
         for h in range(2):
-            nc.vector.tensor_copy(r[:, cols[2 + h]], res_raw[1][:].indirect(offsets[:, h * HALF // 16 : (h + 1) * HALF // 16]))
+            nc.vector.tensor_copy(r_rest[:, cols[2 + h]], res1_raw[:].indirect(entries(halves[h])))
+        r = [r_first[:]] + [r_rest[:, c] for c in cols[1:]]
+
         d = sb("d", [P, BLOCKS * S], F32, on="w2b_grouped")
-        nc.gpsimd.tensor_tensor(d[:, cols[0]], y_first[:], r_first[:], ALU.subtract)
-        for c in (slice(HALF, 3 * HALF), cols[3]):
-            nc.vector.tensor_tensor(d[:, c], y_rest[:, c.start - HALF : c.stop - HALF], r[:, c], ALU.subtract)
+        nc.gpsimd.tensor_tensor(d[:, cols[0]], y[0], r[0], ALU.subtract)
+        nc.vector.tensor_tensor(d[:, HALF : 3 * HALF], y_rest[:, : 2 * HALF], r_rest[:, HALF : 3 * HALF], ALU.subtract)
+        nc.vector.tensor_tensor(d[:, cols[3]], y[3], r[3], ALU.subtract)
+
         th = sb("tanh", [P, BLOCKS * S], F32)
         for i, (b, h) in enumerate(quarters):
             nc.scalar.activation(th[:, cols[i]], g_bank[b][h][:], ACT.Tanh, scale=0.5)
-        e = placed("e", [P, BLOCKS * S], 3 * HALF * 4)
+        e = placed("e", [P, BLOCKS * S], 3 * HALF)
         o = sb("o", [P, BLOCKS * S], F32)
 
         def gate(c):
@@ -216,7 +216,7 @@ def tile_picked_highway_gelu_l_kernel(tc, xT, res, w1, w2, offs, out):
 
         def finish(i):
             b, h = quarters[i]
-            nc.vector.scalar_tensor_tensor(o[:, cols[i]], e[:, cols[i]], 0.5, r[:, cols[i]] if i else r_first[:], ALU.mult, ALU.add)
+            nc.vector.scalar_tensor_tensor(o[:, cols[i]], e[:, cols[i]], 0.5, r[i], ALU.mult, ALU.add)
             nc.sync.dma_start(out[blocks[b], halves[h]], o[:, cols[i]])
 
         gate(slice(0, S))

@@ -22,22 +22,17 @@ PASSES = K // K_PASS
 BLOCKS = N // P
 HALF = S // 2
 GROUP = 16
-F32_BYTES = 4
-VECTOR_COLUMNS = 640
+VECTOR_COLUMNS = (640, 640, 640, 448)
 
 
 def tile_picked_highway_gelu_l_kernel(tc, xT, res, w1, w2, offs, out):
     nc = tc.nc
     with ExitStack() as ctx:
         keep = ctx.enter_context(tc.tile_pool(name="keep", bufs=1))
-        shared = ctx.enter_context(tc.tile_pool(name="shared", bufs=1))
         psum = ctx.enter_context(tc.psum_pool(name="psum", bufs=1))
 
         def sb(name, shape, dtype, on=None):
             return keep.tile(shape, dtype, name=name, tag=on or name, align_bytes=64)
-
-        def placed(name, shape, column):
-            return shared.tile(shape, F32, name=name, offset=column * F32_BYTES, align_bytes=64)
 
         offsets = keep.tile([P, S // GROUP], U16, name="offsets")
         warm_in = sb("warm_in", [P, 1], F32)
@@ -47,10 +42,11 @@ def tile_picked_highway_gelu_l_kernel(tc, xT, res, w1, w2, offs, out):
 
         all_toks = slice(0, S)
         halves = [slice(h * HALF, (h + 1) * HALF) for h in range(2)]
-        all_rows = slice(0, N)
         blocks = [slice(b * P, (b + 1) * P) for b in range(BLOCKS)]
         quarters = [(b, h) for b in range(BLOCKS) for h in range(2)]
-        cols = [slice(i * HALF, (i + 1) * HALF) for i in range(len(quarters))]
+
+        def cols(first, last):
+            return slice(first * HALF, (last + 1) * HALF)
 
         def entries(toks):
             return offsets[:, toks.start // GROUP : toks.stop // GROUP]
@@ -62,167 +58,142 @@ def tile_picked_highway_gelu_l_kernel(tc, xT, res, w1, w2, offs, out):
             nc.sync.dma_start(tile[:], src)
             return tile
 
-        def load_pair(name, g, t):
-            return load(sb(name, [P, 2, T], F32), pass_rows(xT, g)[:, t : t + 2, :])
+        def load_pair(i):
+            g, u = divmod(i, 2)
+            return load(sb(f"x_raw{i}", [P, 2, T], F32), pass_rows(xT, g)[:, 2 * u : 2 * u + 2, :])
 
-        def load_res(b):
-            return load(sb(f"res_raw{b}", [P, T], F32), res[blocks[b], :])
-
-        x_pair0 = load_pair("x_raw0", 0, 0)
+        x_raw = [load_pair(0)]
         nc.sync.dma_start(offsets[:], offs)
-        x_pair1 = load_pair("x_raw1", 0, 2)
-        x_rows = [load(sb(f"x_plane{t}", [P, T], F32), pass_rows(xT, 1)[:, t, :]) for t in range(2)]
-        x_last = load_pair("x_raw3", 1, 2)
-        res0_raw = load_res(0)
-        w1a_raw = load(sb("w1a_raw", [P, PACK, N], F32), pass_rows(w1, 0))
-        w1b_raw = load(sb("w1b_raw", [P, PACK, N], F32), pass_rows(w1, 1))
-        w2a_raw = load(sb("w2a_raw", [P, PACK, N], F32), pass_rows(w2, 0))
-        w2b_raw = load(placed("w2b_raw", [P, PACK, N], 0), pass_rows(w2, 1))
-        res1_raw = load_res(1)
+        x_raw.extend(load_pair(i) for i in range(1, 4))
+        w1_raw = [load(sb(f"w1_raw{g}", [P, PACK, N], F32), pass_rows(w1, g)) for g in range(PASSES)]
+        w2_raw = [load(sb(f"w2_raw{g}", [P, PACK, N], F32), pass_rows(w2, g)) for g in range(PASSES)]
+        res_raw = [load(sb(f"res_raw{b}", [P, T], F32), res[blocks[b], :]) for b in range(BLOCKS)]
 
-        picked = sb("picked0", [P, 2, S], U32)
+        picked = [sb(f"picked{g}", [P, 2, S], U32) for g in range(PASSES)]
         x_codes = [sb(f"x_codes{g}", [P, S], U32) for g in range(PASSES)]
         x_scales = [sb(f"x_scales{g}", [P, S], U8) for g in range(PASSES)]
 
-        def pair_views(name, raw):
-            pairs = sb(name, [P, T, 2], BF16)
-            return pairs, raw[:].rearrange("p e c -> p c e"), pairs[:].rearrange("p c e -> p (c e)").bitcast(U32)
+        def round_pair(i):
+            pairs = sb(f"pairs{i}", [P, T, 2], BF16)
+            src = x_raw[i][:].rearrange("p e c -> p c e")
+            split = VECTOR_COLUMNS[i]
+            nc.scalar.copy(pairs[:, split:, :], src[:, split:, :])
+            nc.vector.tensor_copy(pairs[:, :split, :], src[:, :split, :])
+            return pairs[:].rearrange("p c e -> p (c e)").bitcast(U32)
 
-        def round_pair_shared(name, raw):
-            pairs, src, words = pair_views(name, raw)
-            nc.scalar.copy(pairs[:, VECTOR_COLUMNS:, :], src[:, VECTOR_COLUMNS:, :])
-            nc.vector.tensor_copy(pairs[:, :VECTOR_COLUMNS, :], src[:, :VECTOR_COLUMNS, :])
-            return words
+        def gather_pair(i, words, pieces):
+            g, u = divmod(i, 2)
+            for toks in pieces:
+                nc.vector.tensor_copy(picked[g][:, u, toks], words.indirect(entries(toks)))
 
-        def quant_x(g, woven, toks):
-            nc.vector.quantize_mx(
-                out=x_codes[g][:, toks].bitcast(FP8X4),
-                scales=x_scales[g][:, toks],
-                in_=woven[:, toks.start * PACK : toks.stop * PACK],
-            )
+        def weave(copy, dtype, g, woven):
+            dst = woven[:].bitcast(dtype).rearrange("p (s u) -> p s u", u=2)
+            src = picked[g][:].bitcast(dtype).rearrange("p u s -> p s u")
+            for toks in halves:
+                copy(dst[:, toks, :], src[:, toks, :])
 
-        def w_tiles(name):
+        def quant_x(g, woven):
+            for toks in halves:
+                nc.vector.quantize_mx(
+                    out=x_codes[g][:, toks].bitcast(FP8X4),
+                    scales=x_scales[g][:, toks],
+                    in_=woven[:, toks.start * PACK : toks.stop * PACK],
+                )
+
+        def w_tiles(name, width):
             return (
-                sb(name + "_grouped", [P, N, PACK], BF16),
-                sb(name + "_codes", [P, N], U32),
-                sb(name + "_scales", [P, N], U8),
+                sb(name + "_grouped", [P, width, PACK], BF16),
+                sb(name + "_codes", [P, width], U32),
+                sb(name + "_scales", [P, width], U8),
             )
 
-        def round_w(copy, tiles, raw, rows):
+        def round_w(copy, tiles, at, raw, rows):
+            dst = slice(at + rows.start, at + rows.stop)
             copy(
-                tiles[0][:, rows, :].rearrange("p (c i) t -> p c t i", i=4),
+                tiles[0][:, dst, :].rearrange("p (c i) t -> p c t i", i=4),
                 raw[:, :, rows].rearrange("p t (c i) -> p c t i", i=4),
             )
 
-        def quant_w(tiles, rows):
+        def quant_w(tiles, c):
             nc.vector.quantize_mx(
-                out=tiles[1][:, rows].bitcast(FP8X4),
-                scales=tiles[2][:, rows],
-                in_=tiles[0][:, rows, :].rearrange("p m t -> p (m t)"),
+                out=tiles[1][:, c].bitcast(FP8X4),
+                scales=tiles[2][:, c],
+                in_=tiles[0][:, c, :].rearrange("p m t -> p (m t)"),
             )
 
-        def multiply(banks, tiles, g):
-            for b, h in quarters:
+        def multiply(banks, tiles, at, g):
+            for i, (b, h) in enumerate(quarters):
+                c = slice(at + blocks[b].start, at + blocks[b].stop)
                 nc.tensor.matmul_mx(
-                    out=banks[b][h][:],
-                    lhsT=tiles[1][:, blocks[b]].bitcast(FP8X4),
-                    lhsT_scale=tiles[2][:, blocks[b]],
+                    out=banks[i][:],
+                    lhsT=tiles[1][:, c].bitcast(FP8X4),
+                    lhsT_scale=tiles[2][:, c],
                     rhs=x_codes[g][:, halves[h]].bitcast(FP8X4),
                     rhs_scale=x_scales[g][:, halves[h]],
                     start=(g == 0),
                     stop=(g == PASSES - 1),
                 )
 
-        y_bank = [[psum.tile([P, HALF], F32, name=f"y_bank{b}{h}") for h in range(2)] for b in range(BLOCKS)]
-        g_bank = [[psum.tile([P, HALF], F32, name=f"g_bank{b}{h}") for h in range(2)] for b in range(BLOCKS)]
+        y_bank = [psum.tile([P, HALF], F32, name=f"y_bank{i}") for i in range(4)]
+        g_bank = [psum.tile([P, HALF], F32, name=f"g_bank{i}") for i in range(4)]
 
-        words = round_pair_shared("pairs0", x_pair0)
-        nc.vector.tensor_copy(picked[:, 0, all_toks], words.indirect(entries(all_toks)))
-        words = round_pair_shared("pairs1", x_pair1)
-        for toks in halves:
-            nc.vector.tensor_copy(picked[:, 1, toks], words.indirect(entries(toks)))
+        gather_pair(0, round_pair(0), [all_toks])
+        gather_pair(1, round_pair(1), [all_toks])
+        gather_pair(2, round_pair(2), [all_toks])
+        woven0 = sb("woven0", [P, S * PACK], BF16, on="x_raw2")
+        weave(nc.scalar.copy, U32, 0, woven0)
+        quant_x(0, woven0)
+        gather_pair(3, round_pair(3), [all_toks])
 
-        planes = [sb(f"plane{t}", [P, T], BF16) for t in range(2)]
-        nc.scalar.copy(planes[0][:], x_rows[0][:])
-        for c in (slice(0, T // 2), slice(T // 2, T)):
-            nc.vector.tensor_copy(planes[1][:, c], x_rows[1][:, c])
-        woven1 = sb("woven1", [P, S * PACK], BF16)
-        by_slot = woven1[:].rearrange("p (s t) -> p t s", t=PACK)
-        for t in range(2):
-            nc.scalar.activation(by_slot[:, t, :], planes[t][:].indirect(offsets[:]), ACT.Copy)
+        w1a = w_tiles("w1a", N)
+        round_w(nc.scalar.copy, w1a, 0, w1_raw[0], slice(0, N))
+        quant_w(w1a, slice(0, N))
+        multiply(y_bank, w1a, 0, 0)
+        woven1 = sb("woven1", [P, S * PACK], BF16, on="w1_raw0")
+        weave(nc.vector.tensor_copy, I32, 1, woven1)
+        quant_x(1, woven1)
+        w1b = w_tiles("w1b", N)
+        round_w(nc.scalar.copy, w1b, 0, w1_raw[1], slice(0, N))
+        quant_w(w1b, slice(0, N))
+        multiply(y_bank, w1b, 0, 1)
 
-        woven0 = x_rows[1][:].bitcast(BF16)
-        woven0_words = woven0.bitcast(I32).rearrange("p (s u) -> p s u", u=2)
-        picked_words = picked[:].bitcast(I32).rearrange("p u s -> p s u")
-        for toks in halves:
-            nc.vector.tensor_copy(woven0_words[:, toks, :], picked_words[:, toks, :])
-        for toks in halves:
-            quant_x(0, woven0, toks)
+        w2t = w_tiles("w2", PASSES * N)
+        for rows in blocks:
+            round_w(nc.scalar.copy, w2t, 0, w2_raw[0], rows)
+        quant_w(w2t, slice(0, P))
+        for rows in blocks:
+            round_w(nc.vector.tensor_copy, w2t, N, w2_raw[1], rows)
+        quant_w(w2t, slice(P, 3 * P))
+        quant_w(w2t, slice(3 * P, 4 * P))
+        multiply(g_bank, w2t, 0, 0)
+        multiply(g_bank, w2t, N, 1)
 
-        pairs, src, words = pair_views("pairs3", x_last)
-        nc.vector.tensor_copy(pairs[:, :T, :], src[:, :T, :])
-        r_first = sb("r_first", [P, HALF], F32)
-        nc.vector.tensor_copy(r_first[:], res0_raw[:].indirect(entries(halves[0])))
-        by_word = woven1[:].bitcast(U32).rearrange("p (s u) -> p u s", u=2)
-        for toks in halves:
-            nc.vector.tensor_copy(by_word[:, 1, toks], words.indirect(entries(toks)))
-
-        w1a = w_tiles("w1a")
-        round_w(nc.scalar.copy, w1a, w1a_raw, all_rows)
-        quant_w(w1a, all_rows)
-        multiply(y_bank, w1a, 0)
-        r_rest = sb("r_rest", [P, BLOCKS * S], F32, on="w1a_raw")
-        nc.vector.tensor_copy(r_rest[:, cols[1]], res0_raw[:].indirect(entries(halves[1])))
-        w1b = w_tiles("w1b")
-        round_w(nc.scalar.copy, w1b, w1b_raw, all_rows)
-        quant_x(1, woven1, halves[0])
-        quant_w(w1b, all_rows)
-        quant_x(1, woven1, halves[1])
-        multiply(y_bank, w1b, 1)
-
-        w2a = w_tiles("w2a")
-        round_w(nc.scalar.copy, w2a, w2a_raw, all_rows)
-        w2b = w_tiles("w2b")
-        round_w(nc.vector.tensor_copy, w2b, w2b_raw, blocks[0])
-        round_w(nc.scalar.copy, w2b, w2b_raw, blocks[1])
-        quant_w(w2a, all_rows)
-        multiply(g_bank, w2a, 0)
-        for b in range(BLOCKS):
-            quant_w(w2b, blocks[b])
-        multiply(g_bank, w2b, 1)
-
-        y_first = placed("y_first", [P, HALF], 3 * HALF)
-        y_rest = placed("y_rest", [P, 3 * HALF], 0)
-        y = [y_first[:]] + [y_rest[:, c] for c in cols[:3]]
-        for i, (b, h) in enumerate(quarters):
-            nc.scalar.activation(y[i], y_bank[b][h][:], ACT.Gelu_apprx_tanh)
-        for h in range(2):
-            nc.vector.tensor_copy(r_rest[:, cols[2 + h]], res1_raw[:].indirect(entries(halves[h])))
-        r = [r_first[:]] + [r_rest[:, c] for c in cols[1:]]
-
-        d = sb("d", [P, BLOCKS * S], F32, on="w2b_grouped")
-        nc.gpsimd.tensor_tensor(d[:, cols[0]], y[0], r[0], ALU.subtract)
-        nc.vector.tensor_tensor(d[:, HALF : 3 * HALF], y_rest[:, : 2 * HALF], r_rest[:, HALF : 3 * HALF], ALU.subtract)
-        nc.vector.tensor_tensor(d[:, cols[3]], y[3], r[3], ALU.subtract)
-
+        y = sb("y", [P, BLOCKS * S], F32)
+        for i in range(4):
+            nc.scalar.activation(y[:, cols(i, i)], y_bank[i][:], ACT.Gelu_apprx_tanh)
         th = sb("tanh", [P, BLOCKS * S], F32)
-        for i, (b, h) in enumerate(quarters):
-            nc.scalar.activation(th[:, cols[i]], g_bank[b][h][:], ACT.Tanh, scale=0.5)
-        e = placed("e", [P, BLOCKS * S], 3 * HALF)
+        for i in range(4):
+            nc.scalar.activation(th[:, cols(i, i)], g_bank[i][:], ACT.Tanh, scale=-0.5)
+
+        d = sb("d", [P, BLOCKS * S], F32)
+        e = sb("e", [P, BLOCKS * S], F32)
         o = sb("o", [P, BLOCKS * S], F32)
+
+        def diff(i):
+            b, h = quarters[i]
+            c = cols(i, i)
+            nc.vector.tensor_tensor(d[:, c], res_raw[b][:].indirect(entries(halves[h])), y[:, c], ALU.subtract)
 
         def gate(c):
             nc.vector.scalar_tensor_tensor(e[:, c], th[:, c], 1.0, d[:, c], ALU.add, ALU.mult)
 
-        def finish(i):
-            b, h = quarters[i]
-            nc.vector.scalar_tensor_tensor(o[:, cols[i]], e[:, cols[i]], 0.5, r[i], ALU.mult, ALU.add)
-            nc.sync.dma_start(out[blocks[b], halves[h]], o[:, cols[i]])
+        def finish(c, dst):
+            nc.vector.scalar_tensor_tensor(o[:, c], e[:, c], 0.5, y[:, c], ALU.mult, ALU.add)
+            nc.sync.dma_start(dst, o[:, c])
 
-        gate(slice(0, S))
-        gate(cols[2])
-        finish(0)
-        finish(1)
-        gate(cols[3])
-        finish(2)
-        finish(3)
+        for i in range(4):
+            diff(i)
+        gate(cols(0, 2))
+        gate(cols(3, 3))
+        for i, (b, h) in enumerate(quarters):
+            finish(cols(i, i), out[blocks[b], halves[h]])

@@ -22,7 +22,9 @@ PASSES = K // K_PASS
 BLOCKS = N // P
 HALF = S // 2
 GROUP = 16
-VECTOR_COLUMNS = (640, 640, 640, 448)
+LAP = 16
+EARLY = 160
+VECTOR_COLUMNS = (640, 640, 640, 624)
 
 
 def tile_picked_highway_gelu_l_kernel(tc, xT, res, w1, w2, offs, out):
@@ -58,47 +60,54 @@ def tile_picked_highway_gelu_l_kernel(tc, xT, res, w1, w2, offs, out):
             nc.sync.dma_start(tile[:], src)
             return tile
 
-        def load_pair(i):
+        def load_pair(tile, i):
             g, u = divmod(i, 2)
-            return load(sb(f"x_raw{i}", [P, 2, T], F32), pass_rows(xT, g)[:, 2 * u : 2 * u + 2, :])
+            raw = tile.rearrange("p (e c) -> p e c", e=2)
+            nc.sync.dma_start(raw, pass_rows(xT, g)[:, 2 * u : 2 * u + 2, :])
+            return raw
 
-        x_raw = [load_pair(0)]
+        x_raw = [load_pair(sb("x_raw0", [P, 2 * T], F32)[:], 0)]
         nc.sync.dma_start(offsets[:], offs)
-        x_raw.extend(load_pair(i) for i in range(1, 4))
+        x_raw.append(load_pair(sb("x_raw1", [P, 2 * T], F32)[:], 1))
+        x_late = sb("x_late", [P, PACK * T], F32)
+        x_raw.extend(load_pair(x_late[:, 2 * u * T : 2 * (u + 1) * T], 2 + u) for u in range(2))
         w1_raw = [load(sb(f"w1_raw{g}", [P, PACK, N], F32), pass_rows(w1, g)) for g in range(PASSES)]
         w2_raw = [load(sb(f"w2_raw{g}", [P, PACK, N], F32), pass_rows(w2, g)) for g in range(PASSES)]
         res_raw = [load(sb(f"res_raw{b}", [P, T], F32), res[blocks[b], :]) for b in range(BLOCKS)]
 
         picked = [sb(f"picked{g}", [P, 2, S], U32) for g in range(PASSES)]
-        x_codes = [sb(f"x_codes{g}", [P, S], U32) for g in range(PASSES)]
-        x_scales = [sb(f"x_scales{g}", [P, S], U8) for g in range(PASSES)]
+        late = {(1, 1): "w1_raw1"}
+        x_codes = [[sb(f"x_codes{g}{h}", [P, HALF], U32, on=late.get((g, h))) for h in range(2)] for g in range(PASSES)]
+        x_scales = [[sb(f"x_scales{g}{h}", [P, HALF], U8) for h in range(2)] for g in range(PASSES)]
 
-        def round_pair(i):
+        def round_pair(i, early=0):
             pairs = sb(f"pairs{i}", [P, T, 2], BF16)
-            src = x_raw[i][:].rearrange("p e c -> p c e")
-            split = VECTOR_COLUMNS[i]
-            nc.scalar.copy(pairs[:, split:, :], src[:, split:, :])
-            nc.vector.tensor_copy(pairs[:, :split, :], src[:, :split, :])
-            return pairs[:].rearrange("p c e -> p (c e)").bitcast(U32)
+            src = x_raw[i].rearrange("p e c -> p c e")
+            split = T - VECTOR_COLUMNS[i]
+            nc.vector.tensor_copy(pairs[:, split:, :], src[:, split:, :])
+            if early:
+                nc.scalar.copy(pairs[:, :LAP, :], src[:, :LAP, :])
+                nc.scalar.copy(pairs[:, LAP:early, :], src[:, LAP:early, :])
+            return lambda: nc.scalar.copy(pairs[:, early:split, :], src[:, early:split, :]), pairs[:].rearrange(
+                "p c e -> p (c e)"
+            ).bitcast(U32)
 
         def gather_pair(i, words, pieces):
             g, u = divmod(i, 2)
             for toks in pieces:
                 nc.vector.tensor_copy(picked[g][:, u, toks], words.indirect(entries(toks)))
 
-        def weave(copy, dtype, g, woven):
-            dst = woven[:].bitcast(dtype).rearrange("p (s u) -> p s u", u=2)
+        def weave(copy, dtype, g, woven, toks):
+            dst = woven.bitcast(dtype).rearrange("p (s u) -> p s u", u=2)
             src = picked[g][:].bitcast(dtype).rearrange("p u s -> p s u")
-            for toks in halves:
-                copy(dst[:, toks, :], src[:, toks, :])
+            copy(dst[:, toks, :], src[:, toks, :])
 
-        def quant_x(g, woven):
-            for toks in halves:
-                nc.vector.quantize_mx(
-                    out=x_codes[g][:, toks].bitcast(FP8X4),
-                    scales=x_scales[g][:, toks],
-                    in_=woven[:, toks.start * PACK : toks.stop * PACK],
-                )
+        def quant_x(g, h, woven):
+            nc.vector.quantize_mx(
+                out=x_codes[g][h][:].bitcast(FP8X4),
+                scales=x_scales[g][h][:],
+                in_=woven[:, h * HALF * PACK : (h + 1) * HALF * PACK],
+            )
 
         def w_tiles(name, width):
             return (
@@ -128,8 +137,8 @@ def tile_picked_highway_gelu_l_kernel(tc, xT, res, w1, w2, offs, out):
                     out=banks[i][:],
                     lhsT=tiles[1][:, c].bitcast(FP8X4),
                     lhsT_scale=tiles[2][:, c],
-                    rhs=x_codes[g][:, halves[h]].bitcast(FP8X4),
-                    rhs_scale=x_scales[g][:, halves[h]],
+                    rhs=x_codes[g][h][:].bitcast(FP8X4),
+                    rhs_scale=x_scales[g][h][:],
                     start=(g == 0),
                     stop=(g == PASSES - 1),
                 )
@@ -137,24 +146,33 @@ def tile_picked_highway_gelu_l_kernel(tc, xT, res, w1, w2, offs, out):
         y_bank = [psum.tile([P, HALF], F32, name=f"y_bank{i}") for i in range(4)]
         g_bank = [psum.tile([P, HALF], F32, name=f"g_bank{i}") for i in range(4)]
 
-        gather_pair(0, round_pair(0), [all_toks])
-        gather_pair(1, round_pair(1), [all_toks])
-        gather_pair(2, round_pair(2), [all_toks])
-        woven0 = sb("woven0", [P, S * PACK], BF16, on="x_raw2")
-        weave(nc.scalar.copy, U32, 0, woven0)
-        quant_x(0, woven0)
-        gather_pair(3, round_pair(3), [all_toks])
+        for i in range(3):
+            rest, words = round_pair(i)
+            rest()
+            gather_pair(i, words, [all_toks])
+        woven0 = x_late[:, 2 * T + LAP - 2 * S : 2 * T + LAP].bitcast(BF16)
+        last = S - LAP // 2
+        weave(nc.scalar.copy, U32, 0, woven0, halves[0])
+        weave(nc.scalar.copy, U32, 0, woven0, slice(HALF, last))
+        quant_x(0, 0, woven0)
+        rest, words = round_pair(3, EARLY)
+        weave(nc.scalar.copy, U32, 0, woven0, slice(last, S))
+        rest()
+        quant_x(0, 1, woven0)
+        gather_pair(3, words, [all_toks])
 
         w1a = w_tiles("w1a", N)
         round_w(nc.scalar.copy, w1a, 0, w1_raw[0], slice(0, N))
         quant_w(w1a, slice(0, N))
         multiply(y_bank, w1a, 0, 0)
         woven1 = sb("woven1", [P, S * PACK], BF16, on="w1_raw0")
-        weave(nc.vector.tensor_copy, I32, 1, woven1)
-        quant_x(1, woven1)
+        for toks in halves:
+            weave(nc.vector.tensor_copy, I32, 1, woven1[:], toks)
+        quant_x(1, 0, woven1)
         w1b = w_tiles("w1b", N)
         round_w(nc.scalar.copy, w1b, 0, w1_raw[1], slice(0, N))
         quant_w(w1b, slice(0, N))
+        quant_x(1, 1, woven1)
         multiply(y_bank, w1b, 0, 1)
 
         w2t = w_tiles("w2", PASSES * N)

@@ -8,7 +8,6 @@ FLOPS = 2 * 2 * K * S * N
 F32 = mybir.dt.float32
 BF16 = mybir.dt.bfloat16
 U32 = mybir.dt.uint32
-I32 = mybir.dt.int32
 U16 = mybir.dt.uint16
 U8 = mybir.dt.uint8
 FP8X4 = mybir.dt.float8_e4m3fn_x4
@@ -22,9 +21,7 @@ PASSES = K // K_PASS
 BLOCKS = N // P
 HALF = S // 2
 GROUP = 16
-LAP = 16
-EARLY = 160
-VECTOR_COLUMNS = (640, 640, 640, 624)
+QUARTER = S // 4
 
 
 def tile_picked_highway_gelu_l_kernel(tc, xT, res, w1, w2, offs, out):
@@ -60,158 +57,162 @@ def tile_picked_highway_gelu_l_kernel(tc, xT, res, w1, w2, offs, out):
             nc.sync.dma_start(tile[:], src)
             return tile
 
-        def load_pair(tile, i):
-            g, u = divmod(i, 2)
-            raw = tile.rearrange("p (e c) -> p e c", e=2)
-            nc.sync.dma_start(raw, pass_rows(xT, g)[:, 2 * u : 2 * u + 2, :])
-            return raw
+        def load_rows(g, first, count):
+            tile = sb(f"x_raw{g}{first}", [P, count * T], F32)
+            nc.sync.dma_start(
+                tile[:].rearrange("p (e c) -> p e c", e=count), pass_rows(xT, g)[:, first : first + count, :]
+            )
+            return [tile[:, e * T : (e + 1) * T] for e in range(count)]
 
-        x_raw = [load_pair(sb("x_raw0", [P, 2 * T], F32)[:], 0)]
+        x_rows = load_rows(0, 0, 2)
         nc.sync.dma_start(offsets[:], offs)
-        x_raw.append(load_pair(sb("x_raw1", [P, 2 * T], F32)[:], 1))
-        x_late = sb("x_late", [P, PACK * T], F32)
-        x_raw.extend(load_pair(x_late[:, 2 * u * T : 2 * (u + 1) * T], 2 + u) for u in range(2))
+        x_rows.extend(load_rows(0, 2, 1))
+        x_rows.extend(load_rows(0, 3, 1))
+        x_rows.extend(load_rows(1, 0, 2))
+        x_rows.extend(load_rows(1, 2, 1))
+        x_rows.extend(load_rows(1, 3, 1))
         w1_raw = [load(sb(f"w1_raw{g}", [P, PACK, N], F32), pass_rows(w1, g)) for g in range(PASSES)]
         w2_raw = [load(sb(f"w2_raw{g}", [P, PACK, N], F32), pass_rows(w2, g)) for g in range(PASSES)]
         res_raw = [load(sb(f"res_raw{b}", [P, T], F32), res[blocks[b], :]) for b in range(BLOCKS)]
 
-        picked = [sb(f"picked{g}", [P, 2, S], U32) for g in range(PASSES)]
-        late = {(1, 1): "w1_raw1"}
-        x_codes = [[sb(f"x_codes{g}{h}", [P, HALF], U32, on=late.get((g, h))) for h in range(2)] for g in range(PASSES)]
-        x_scales = [[sb(f"x_scales{g}{h}", [P, HALF], U8) for h in range(2)] for g in range(PASSES)]
+        picked = [sb(f"picked{g}", [P, PACK * S], F32) for g in range(PASSES)]
 
-        def round_pair(i, early=0):
-            pairs = sb(f"pairs{i}", [P, T, 2], BF16)
-            src = x_raw[i].rearrange("p e c -> p c e")
-            split = T - VECTOR_COLUMNS[i]
-            nc.vector.tensor_copy(pairs[:, split:, :], src[:, split:, :])
-            if early:
-                nc.scalar.copy(pairs[:, :LAP, :], src[:, :LAP, :])
-                nc.scalar.copy(pairs[:, LAP:early, :], src[:, LAP:early, :])
-            return lambda: nc.scalar.copy(pairs[:, early:split, :], src[:, early:split, :]), pairs[:].rearrange(
-                "p c e -> p (c e)"
-            ).bitcast(U32)
+        def picked_row(row, toks):
+            g, t = divmod(row, PACK)
+            return picked[g][:, t * S + toks.start : t * S + toks.stop]
 
-        def gather_pair(i, words, pieces):
-            g, u = divmod(i, 2)
-            for toks in pieces:
-                nc.vector.tensor_copy(picked[g][:, u, toks], words.indirect(entries(toks)))
+        def gather_on_vector(row, toks):
+            nc.vector.tensor_copy(picked_row(row, toks), x_rows[row].indirect(entries(toks)))
 
-        def weave(copy, dtype, g, woven, toks):
-            dst = woven.bitcast(dtype).rearrange("p (s u) -> p s u", u=2)
-            src = picked[g][:].bitcast(dtype).rearrange("p u s -> p s u")
-            copy(dst[:, toks, :], src[:, toks, :])
+        def gather_on_scalar(row, toks):
+            nc.scalar.activation(picked_row(row, toks), x_rows[row].indirect(entries(toks)), ACT.Copy)
 
-        def quant_x(g, h, woven):
-            nc.vector.quantize_mx(
-                out=x_codes[g][h][:].bitcast(FP8X4),
-                scales=x_scales[g][h][:],
-                in_=woven[:, h * HALF * PACK : (h + 1) * HALF * PACK],
-            )
+        def batch(name, widths):
+            total = sum(widths)
+            grouped = sb(name + "_grouped", [P, total, PACK], BF16)
+            codes = sb(name + "_codes", [P, total], U32)
+            scales = sb(name + "_scales", [P, total], U8)
+            starts = [sum(widths[:i]) for i in range(len(widths))]
+            parts = [slice(a, a + n) for a, n in zip(starts, widths)]
 
-        def w_tiles(name, width):
-            return (
-                sb(name + "_grouped", [P, width, PACK], BF16),
-                sb(name + "_codes", [P, width], U32),
-                sb(name + "_scales", [P, width], U8),
-            )
-
-        def round_w(copy, tiles, at, raw, rows):
-            dst = slice(at + rows.start, at + rows.stop)
-            copy(
-                tiles[0][:, dst, :].rearrange("p (c i) t -> p c t i", i=4),
-                raw[:, :, rows].rearrange("p t (c i) -> p c t i", i=4),
-            )
-
-        def quant_w(tiles, c):
-            nc.vector.quantize_mx(
-                out=tiles[1][:, c].bitcast(FP8X4),
-                scales=tiles[2][:, c],
-                in_=tiles[0][:, c, :].rearrange("p m t -> p (m t)"),
-            )
-
-        def multiply(banks, tiles, at, g):
-            for i, (b, h) in enumerate(quarters):
-                c = slice(at + blocks[b].start, at + blocks[b].stop)
-                nc.tensor.matmul_mx(
-                    out=banks[i][:],
-                    lhsT=tiles[1][:, c].bitcast(FP8X4),
-                    lhsT_scale=tiles[2][:, c],
-                    rhs=x_codes[g][h][:].bitcast(FP8X4),
-                    rhs_scale=x_scales[g][h][:],
-                    start=(g == 0),
-                    stop=(g == PASSES - 1),
+            def quantise():
+                nc.vector.quantize_mx(
+                    out=codes[:].bitcast(FP8X4), scales=scales[:], in_=grouped[:].rearrange("p m t -> p (m t)")
                 )
+
+            return quantise, [(grouped[:, c, :], codes[:, c].bitcast(FP8X4), scales[:, c]) for c in parts]
+
+        def interleave(copy, dst, src):
+            copy(dst.rearrange("p (c i) t -> p c t i", i=4), src.rearrange("p t (c i) -> p c t i", i=4))
+
+        def weave(copy, g, part, first, toks):
+            src = picked[g][:].rearrange("p (t s) -> p t s", t=PACK)
+            interleave(copy, part[0][:, toks.start - first : toks.stop - first, :], src[:, :, toks])
+
+        def round_w(copy, part, raw, b):
+            interleave(copy, part[0], raw[:, :, blocks[b]])
+
+        def multiply(bank, w_part, x_part, g):
+            nc.tensor.matmul_mx(
+                out=bank[:],
+                lhsT=w_part[1],
+                lhsT_scale=w_part[2],
+                rhs=x_part[1],
+                rhs_scale=x_part[2],
+                start=(g == 0),
+                stop=(g == PASSES - 1),
+            )
 
         y_bank = [psum.tile([P, HALF], F32, name=f"y_bank{i}") for i in range(4)]
         g_bank = [psum.tile([P, HALF], F32, name=f"g_bank{i}") for i in range(4)]
 
-        for i in range(3):
-            rest, words = round_pair(i)
-            rest()
-            gather_pair(i, words, [all_toks])
-        woven0 = x_late[:, 2 * T + LAP - 2 * S : 2 * T + LAP].bitcast(BF16)
-        last = S - LAP // 2
-        weave(nc.scalar.copy, U32, 0, woven0, halves[0])
-        weave(nc.scalar.copy, U32, 0, woven0, slice(HALF, last))
-        quant_x(0, 0, woven0)
-        rest, words = round_pair(3, EARLY)
-        weave(nc.scalar.copy, U32, 0, woven0, slice(last, S))
-        rest()
-        quant_x(0, 1, woven0)
-        gather_pair(3, words, [all_toks])
+        quant_0, (x00,) = batch("q0", [HALF])
+        quant_1, (x01,) = batch("q1", [HALF])
+        quant_2, (w1a0, x10) = batch("q2", [P, HALF])
+        quant_3, (w1a1, x11) = batch("q3", [P, HALF])
+        quant_4, (w1b0,) = batch("q4", [P])
+        quant_5, (w1b1, w2a0) = batch("q5", [P, P])
+        quant_6, (w2b0,) = batch("q6", [P])
+        quant_7, (w2a1, w2b1) = batch("q7", [P, P])
+        x_parts = [[x00, x01], [x10, x11]]
 
-        w1a = w_tiles("w1a", N)
-        round_w(nc.scalar.copy, w1a, 0, w1_raw[0], slice(0, N))
-        quant_w(w1a, slice(0, N))
-        multiply(y_bank, w1a, 0, 0)
-        woven1 = sb("woven1", [P, S * PACK], BF16, on="w1_raw0")
-        for toks in halves:
-            weave(nc.vector.tensor_copy, I32, 1, woven1[:], toks)
-        quant_x(1, 0, woven1)
-        w1b = w_tiles("w1b", N)
-        round_w(nc.scalar.copy, w1b, 0, w1_raw[1], slice(0, N))
-        quant_w(w1b, slice(0, N))
-        quant_x(1, 1, woven1)
-        multiply(y_bank, w1b, 0, 1)
+        def products(banks, w_part, g, b):
+            for h in range(2):
+                multiply(banks[2 * b + h], w_part, x_parts[g][h], g)
 
-        w2t = w_tiles("w2", PASSES * N)
-        for rows in blocks:
-            round_w(nc.scalar.copy, w2t, 0, w2_raw[0], rows)
-        quant_w(w2t, slice(0, P))
-        for rows in blocks:
-            round_w(nc.vector.tensor_copy, w2t, N, w2_raw[1], rows)
-        quant_w(w2t, slice(P, 3 * P))
-        quant_w(w2t, slice(3 * P, 4 * P))
-        multiply(g_bank, w2t, 0, 0)
-        multiply(g_bank, w2t, N, 1)
+        def share(row, split):
+            gather_on_vector(row, slice(0, split))
+            gather_on_scalar(row, slice(split, S))
+
+        def last_row(g):
+            row = PACK * g + PACK - 1
+            gather_on_vector(row, slice(0, QUARTER))
+            gather_on_scalar(row, slice(QUARTER, HALF))
+            gather_on_scalar(row, halves[1])
+            for h in range(2):
+                weave(nc.vector.tensor_copy, g, x_parts[g][h], halves[h].start, halves[h])
+
+        gather_on_vector(0, all_toks)
+        gather_on_scalar(1, all_toks)
+        share(2, HALF)
+        last_row(0)
+        quant_0()
+        quant_1()
+        gather_on_vector(4, all_toks)
+        gather_on_scalar(5, all_toks)
+        share(6, QUARTER)
+        last_row(1)
+
+        round_w(nc.scalar.copy, w1a0, w1_raw[0], 0)
+        quant_2()
+        products(y_bank, w1a0, 0, 0)
+        round_w(nc.scalar.copy, w1a1, w1_raw[0], 1)
+        quant_3()
+        products(y_bank, w1a1, 0, 1)
+        round_w(nc.scalar.copy, w1b0, w1_raw[1], 0)
+        quant_4()
+        products(y_bank, w1b0, 1, 0)
+        round_w(nc.scalar.copy, w1b1, w1_raw[1], 1)
+        round_w(nc.vector.tensor_copy, w2a0, w2_raw[0], 0)
+        round_w(nc.scalar.copy, w2a1, w2_raw[0], 1)
+        quant_5()
+        products(y_bank, w1b1, 1, 1)
+        products(g_bank, w2a0, 0, 0)
+        round_w(nc.vector.tensor_copy, w2b0, w2_raw[1], 0)
+        round_w(nc.vector.tensor_copy, w2b1, w2_raw[1], 1)
+        quant_6()
+        products(g_bank, w2b0, 1, 0)
+        quant_7()
+        products(g_bank, w2a1, 0, 1)
+        products(g_bank, w2b1, 1, 1)
 
         y = sb("y", [P, BLOCKS * S], F32)
         for i in range(4):
             nc.scalar.activation(y[:, cols(i, i)], y_bank[i][:], ACT.Gelu_apprx_tanh)
-        th = sb("tanh", [P, BLOCKS * S], F32)
-        for i in range(4):
-            nc.scalar.activation(th[:, cols(i, i)], g_bank[i][:], ACT.Tanh, scale=-0.5)
 
+        r = sb("r", [P, BLOCKS * S], F32)
         d = sb("d", [P, BLOCKS * S], F32)
         e = sb("e", [P, BLOCKS * S], F32)
         o = sb("o", [P, BLOCKS * S], F32)
 
-        def diff(i):
+        def window(i):
             b, h = quarters[i]
-            c = cols(i, i)
-            nc.vector.tensor_tensor(d[:, c], res_raw[b][:].indirect(entries(halves[h])), y[:, c], ALU.subtract)
+            return res_raw[b][:].indirect(entries(halves[h]))
 
-        def gate(c):
-            nc.vector.scalar_tensor_tensor(e[:, c], th[:, c], 1.0, d[:, c], ALU.add, ALU.mult)
-
-        def finish(c, dst):
-            nc.vector.scalar_tensor_tensor(o[:, c], e[:, c], 0.5, y[:, c], ALU.mult, ALU.add)
-            nc.sync.dma_start(dst, o[:, c])
-
-        for i in range(4):
-            diff(i)
-        gate(cols(0, 2))
-        gate(cols(3, 3))
-        for i, (b, h) in enumerate(quarters):
-            finish(cols(i, i), out[blocks[b], halves[h]])
+        for i in range(2):
+            nc.vector.tensor_tensor(d[:, cols(i, i)], window(i), y[:, cols(i, i)], ALU.subtract)
+        for i in range(2, 4):
+            nc.scalar.activation(r[:, cols(i, i)], window(i), ACT.Copy)
+        for b in range(BLOCKS):
+            th = sb(f"tanh{b}", [P, S], F32, on=f"res_raw{b}" if b else None)
+            for h in range(2):
+                nc.scalar.activation(th[:, halves[h]], g_bank[2 * b + h][:], ACT.Tanh, scale=-0.5)
+            both = [cols(2 * b + h, 2 * b + h) for h in range(2)]
+            for h in range(2):
+                if b > 0:
+                    nc.vector.tensor_tensor(d[:, both[h]], r[:, both[h]], y[:, both[h]], ALU.subtract)
+            for h in range(2):
+                nc.vector.scalar_tensor_tensor(e[:, both[h]], th[:, halves[h]], 1.0, d[:, both[h]], ALU.add, ALU.mult)
+            for h in range(2):
+                nc.vector.scalar_tensor_tensor(o[:, both[h]], e[:, both[h]], 0.5, y[:, both[h]], ALU.mult, ALU.add)
+                nc.sync.dma_start(out[blocks[b], halves[h]], o[:, both[h]])

@@ -124,16 +124,15 @@ def tile_picked_highway_gelu_l_kernel(tc, xT, res, w1, w2, offs, out):
             )
 
         y_bank = [psum.tile([P, HALF], F32, name=f"y_bank{i}") for i in range(4)]
-        g_bank = [psum.tile([P, HALF], F32, name=f"g_bank{i}") for i in range(4)]
 
         quant_0, (x00,) = batch("q0", [HALF])
         quant_1, (x01,) = batch("q1", [HALF])
         quant_2, (w1a0, x10) = batch("q2", [P, HALF])
         quant_3, (w1a1, x11) = batch("q3", [P, HALF])
-        quant_4, (w1b0,) = batch("q4", [P])
-        quant_5, (w1b1, w2a0) = batch("q5", [P, P])
+        quant_4, (w1b0, w1b1) = batch("q4", [P, P])
+        quant_5, (w2a0, w2a1) = batch("q5", [P, P])
         quant_6, (w2b0,) = batch("q6", [P])
-        quant_7, (w2a1, w2b1) = batch("q7", [P, P])
+        quant_7, (w2b1,) = batch("q7", [P])
         x_parts = [[x00, x01], [x10, x11]]
 
         def products(banks, w_part, g, b):
@@ -170,21 +169,18 @@ def tile_picked_highway_gelu_l_kernel(tc, xT, res, w1, w2, offs, out):
         quant_3()
         products(y_bank, w1a1, 0, 1)
         round_w(nc.scalar.copy, w1b0, w1_raw[1], 0)
+        round_w(nc.vector.tensor_copy, w1b1, w1_raw[1], 1)
         quant_4()
         products(y_bank, w1b0, 1, 0)
-        round_w(nc.scalar.copy, w1b1, w1_raw[1], 1)
-        round_w(nc.vector.tensor_copy, w2a0, w2_raw[0], 0)
-        round_w(nc.scalar.copy, w2a1, w2_raw[0], 1)
-        quant_5()
         products(y_bank, w1b1, 1, 1)
-        products(g_bank, w2a0, 0, 0)
+        round_w(nc.scalar.copy, w2a0, w2_raw[0], 0)
+        round_w(nc.vector.tensor_copy, w2a1, w2_raw[0], 1)
+        quant_5()
         round_w(nc.vector.tensor_copy, w2b0, w2_raw[1], 0)
         round_w(nc.vector.tensor_copy, w2b1, w2_raw[1], 1)
         quant_6()
-        products(g_bank, w2b0, 1, 0)
         quant_7()
-        products(g_bank, w2a1, 0, 1)
-        products(g_bank, w2b1, 1, 1)
+        w2_parts = [[w2a0, w2a1], [w2b0, w2b1]]
 
         y = sb("y", [P, BLOCKS * S], F32)
         for i in range(4):
@@ -192,7 +188,6 @@ def tile_picked_highway_gelu_l_kernel(tc, xT, res, w1, w2, offs, out):
 
         r = sb("r", [P, BLOCKS * S], F32)
         d = sb("d", [P, BLOCKS * S], F32)
-        e = sb("e", [P, BLOCKS * S], F32)
         o = sb("o", [P, BLOCKS * S], F32)
 
         def window(i):
@@ -204,15 +199,20 @@ def tile_picked_highway_gelu_l_kernel(tc, xT, res, w1, w2, offs, out):
         for i in range(2, 4):
             nc.scalar.activation(r[:, cols(i, i)], window(i), ACT.Copy)
         for b in range(BLOCKS):
-            th = sb(f"tanh{b}", [P, S], F32, on=f"res_raw{b}" if b else None)
+            g_bank = [psum.tile([P, HALF], F32, name=f"g_bank{b}{h}", tag=f"g_bank{h}") for h in range(2)]
             for h in range(2):
-                nc.scalar.activation(th[:, halves[h]], g_bank[2 * b + h][:], ACT.Tanh, scale=-0.5)
+                for g in range(PASSES):
+                    multiply(g_bank[h], w2_parts[g][b], x_parts[g][h], g)
             both = [cols(2 * b + h, 2 * b + h) for h in range(2)]
+            th = [sb(f"tanh{b}{h}", [P, HALF], F32, on=f"e0{h}" if b else None) for h in range(2)]
+            for h in range(2):
+                nc.scalar.activation(th[h][:], g_bank[h][:], ACT.Tanh, scale=-0.5)
             for h in range(2):
                 if b > 0:
                     nc.vector.tensor_tensor(d[:, both[h]], r[:, both[h]], y[:, both[h]], ALU.subtract)
+            e = [sb(f"e{b}{h}", [P, HALF], F32) for h in range(2)]
             for h in range(2):
-                nc.vector.scalar_tensor_tensor(e[:, both[h]], th[:, halves[h]], 1.0, d[:, both[h]], ALU.add, ALU.mult)
+                nc.vector.scalar_tensor_tensor(e[h][:], th[h][:], 1.0, d[:, both[h]], ALU.add, ALU.mult)
             for h in range(2):
-                nc.vector.scalar_tensor_tensor(o[:, both[h]], e[:, both[h]], 0.5, y[:, both[h]], ALU.mult, ALU.add)
+                nc.vector.scalar_tensor_tensor(o[:, both[h]], e[h][:], 0.5, y[:, both[h]], ALU.mult, ALU.add)
                 nc.sync.dma_start(out[blocks[b], halves[h]], o[:, both[h]])

@@ -129,7 +129,8 @@ def tile_picked_highway_gelu_l_kernel(tc, xT, res, w1, w2, offs, out):
         quant_1, (x01,) = batch("q1", [HALF])
         quant_2, (w1a0, x10) = batch("q2", [P, HALF])
         quant_3, (w1a1, x11) = batch("q3", [P, HALF])
-        quant_4, (w1b0, w1b1) = batch("q4", [P, P])
+        quant_4a, (w1b0,) = batch("q4a", [P])
+        quant_4b, (w1b1,) = batch("q4b", [P])
         quant_5, (w2a0, w2a1) = batch("q5", [P, P])
         quant_6, (w2b0,) = batch("q6", [P])
         quant_7, (w2b1,) = batch("q7", [P])
@@ -168,13 +169,14 @@ def tile_picked_highway_gelu_l_kernel(tc, xT, res, w1, w2, offs, out):
         round_w(nc.scalar.copy, w1a1, w1_raw[0], 1)
         quant_3()
         products(y_bank, w1a1, 0, 1)
-        round_w(nc.scalar.copy, w1b0, w1_raw[1], 0)
-        round_w(nc.vector.tensor_copy, w1b1, w1_raw[1], 1)
-        quant_4()
+        round_w(nc.vector.tensor_copy, w1b0, w1_raw[1], 0)
+        round_w(nc.scalar.copy, w1b1, w1_raw[1], 1)
+        quant_4a()
         products(y_bank, w1b0, 1, 0)
+        quant_4b()
         products(y_bank, w1b1, 1, 1)
-        round_w(nc.scalar.copy, w2a0, w2_raw[0], 0)
-        round_w(nc.vector.tensor_copy, w2a1, w2_raw[0], 1)
+        round_w(nc.vector.tensor_copy, w2a0, w2_raw[0], 0)
+        round_w(nc.scalar.copy, w2a1, w2_raw[0], 1)
         quant_5()
         round_w(nc.vector.tensor_copy, w2b0, w2_raw[1], 0)
         round_w(nc.vector.tensor_copy, w2b1, w2_raw[1], 1)

@@ -144,24 +144,26 @@ def tile_picked_highway_gelu_l_kernel(tc, xT, res, w1, w2, offs, out):
             gather_on_vector(row, slice(0, split))
             gather_on_scalar(row, slice(split, S))
 
-        def last_row(g):
+        def last_row(g, split):
             row = PACK * g + PACK - 1
             gather_on_vector(row, slice(0, QUARTER))
             gather_on_scalar(row, slice(QUARTER, HALF))
             gather_on_scalar(row, halves[1])
-            for h in range(2):
-                weave(nc.vector.tensor_copy, g, x_parts[g][h], halves[h].start, halves[h])
+            weave(nc.vector.tensor_copy, g, x_parts[g][0], 0, halves[0])
+            weave(nc.vector.tensor_copy, g, x_parts[g][1], HALF, slice(HALF, split))
+            if split < S:
+                weave(nc.scalar.copy, g, x_parts[g][1], HALF, slice(split, S))
 
         gather_on_vector(0, all_toks)
         gather_on_scalar(1, all_toks)
         share(2, HALF)
-        last_row(0)
+        last_row(0, S - QUARTER)
         quant_0()
         quant_1()
         gather_on_vector(4, all_toks)
         gather_on_scalar(5, all_toks)
-        share(6, QUARTER)
-        last_row(1)
+        share(6, HALF)
+        last_row(1, S)
 
         round_w(nc.scalar.copy, w1a0, w1_raw[0], 0)
         quant_2()
@@ -217,4 +219,7 @@ def tile_picked_highway_gelu_l_kernel(tc, xT, res, w1, w2, offs, out):
                 nc.vector.scalar_tensor_tensor(e[h][:], th[h][:], 1.0, d[:, both[h]], ALU.add, ALU.mult)
             for h in range(2):
                 nc.vector.scalar_tensor_tensor(o[:, both[h]], e[h][:], 0.5, y[:, both[h]], ALU.mult, ALU.add)
-                nc.sync.dma_start(out[blocks[b], halves[h]], o[:, both[h]])
+                if b > 0:
+                    nc.sync.dma_start(out[blocks[b], halves[h]], o[:, both[h]])
+            if b == 0:
+                nc.sync.dma_start(out[blocks[b], :], o[:, cols(0, 1)])

@@ -22,6 +22,7 @@ BLOCKS = N // P
 HALF = S // 2
 GROUP = 16
 QUARTER = S // 4
+RES_SPLIT = 384
 
 
 def tile_picked_highway_gelu_l_kernel(tc, xT, res, w1, w2, offs, out):
@@ -180,10 +181,10 @@ def tile_picked_highway_gelu_l_kernel(tc, xT, res, w1, w2, offs, out):
         round_w(nc.vector.tensor_copy, w2a0, w2_raw[0], 0)
         round_w(nc.scalar.copy, w2a1, w2_raw[0], 1)
         quant_5()
-        round_w(nc.vector.tensor_copy, w2b0, w2_raw[1], 0)
         round_w(nc.vector.tensor_copy, w2b1, w2_raw[1], 1)
-        quant_6()
+        round_w(nc.vector.tensor_copy, w2b0, w2_raw[1], 0)
         quant_7()
+        quant_6()
         w2_parts = [[w2a0, w2a1], [w2b0, w2b1]]
 
         y = sb("y", [P, BLOCKS * S], F32)
@@ -194,26 +195,32 @@ def tile_picked_highway_gelu_l_kernel(tc, xT, res, w1, w2, offs, out):
         d = sb("d", [P, BLOCKS * S], F32)
         o = sb("o", [P, BLOCKS * S], F32)
 
-        def window(i):
-            b, h = quarters[i]
-            return res_raw[b][:].indirect(entries(halves[h]))
+        def span(b, toks):
+            return slice(b * S + toks.start, b * S + toks.stop)
 
-        for i in range(2):
-            nc.vector.tensor_tensor(d[:, cols(i, i)], window(i), y[:, cols(i, i)], ALU.subtract)
-        for i in range(2, 4):
-            nc.scalar.activation(r[:, cols(i, i)], window(i), ACT.Copy)
+        def window(b, toks):
+            return res_raw[b][:].indirect(entries(toks))
+
+        def fused(b, toks):
+            nc.vector.tensor_tensor(d[:, span(b, toks)], window(b, toks), y[:, span(b, toks)], ALU.subtract)
+
+        plain = [[slice(RES_SPLIT, S)], halves]
+        fused(0, slice(0, RES_SPLIT))
+        for b in range(BLOCKS):
+            for toks in plain[b]:
+                nc.scalar.activation(r[:, span(b, toks)], window(b, toks), ACT.Copy)
         for b in range(BLOCKS):
             g_bank = [psum.tile([P, HALF], F32, name=f"g_bank{b}{h}", tag=f"g_bank{h}") for h in range(2)]
             for h in range(2):
                 for g in range(PASSES):
                     multiply(g_bank[h], w2_parts[g][b], x_parts[g][h], g)
             both = [cols(2 * b + h, 2 * b + h) for h in range(2)]
-            th = [sb(f"tanh{b}{h}", [P, HALF], F32, on=f"e0{h}" if b else None) for h in range(2)]
+            th = [sb(f"tanh{b}{h}", [P, HALF], F32, on=("tanh01", "e00")[h] if b else None) for h in range(2)]
             for h in range(2):
                 nc.scalar.activation(th[h][:], g_bank[h][:], ACT.Tanh, scale=-0.5)
-            for h in range(2):
-                if b > 0:
-                    nc.vector.tensor_tensor(d[:, both[h]], r[:, both[h]], y[:, both[h]], ALU.subtract)
+            for toks in plain[b]:
+                c = span(b, toks)
+                nc.vector.tensor_tensor(d[:, c], r[:, c], y[:, c], ALU.subtract)
             e = [sb(f"e{b}{h}", [P, HALF], F32) for h in range(2)]
             for h in range(2):
                 nc.vector.scalar_tensor_tensor(e[h][:], th[h][:], 1.0, d[:, both[h]], ALU.add, ALU.mult)

@@ -132,9 +132,8 @@ def tile_picked_highway_gelu_l_kernel(tc, xT, res, w1, w2, offs, out):
         quant_3, (w1a1, x11) = batch("q3", [P, HALF])
         quant_4a, (w1b0,) = batch("q4a", [P])
         quant_4b, (w1b1,) = batch("q4b", [P])
-        quant_5, (w2a0, w2a1) = batch("q5", [P, P])
-        quant_6, (w2b0,) = batch("q6", [P])
-        quant_7, (w2b1,) = batch("q7", [P])
+        quant_6, (w2a0, w2b0) = batch("q6", [P, P])
+        quant_7, (w2a1, w2b1) = batch("q7", [P, P])
         x_parts = [[x00, x01], [x10, x11]]
 
         def products(banks, w_part, g, b):
@@ -180,11 +179,10 @@ def tile_picked_highway_gelu_l_kernel(tc, xT, res, w1, w2, offs, out):
         products(y_bank, w1b1, 1, 1)
         round_w(nc.vector.tensor_copy, w2a0, w2_raw[0], 0)
         round_w(nc.scalar.copy, w2a1, w2_raw[0], 1)
-        quant_5()
-        round_w(nc.vector.tensor_copy, w2b1, w2_raw[1], 1)
         round_w(nc.vector.tensor_copy, w2b0, w2_raw[1], 0)
-        quant_7()
+        round_w(nc.vector.tensor_copy, w2b1, w2_raw[1], 1)
         quant_6()
+        quant_7()
         w2_parts = [[w2a0, w2a1], [w2b0, w2b1]]
 
         y = sb("y", [P, BLOCKS * S], F32)

@@ -133,7 +133,8 @@ def tile_picked_highway_gelu_l_kernel(tc, xT, res, w1, w2, offs, out):
         quant_4a, (w1b0,) = batch("q4a", [P])
         quant_4b, (w1b1,) = batch("q4b", [P])
         quant_6, (w2a0, w2b0) = batch("q6", [P, P])
-        quant_7, (w2a1, w2b1) = batch("q7", [P, P])
+        quant_5, (w2a1,) = batch("q5", [P])
+        quant_7, (w2b1,) = batch("q7", [P])
         x_parts = [[x00, x01], [x10, x11]]
 
         def products(banks, w_part, g, b):
@@ -177,8 +178,9 @@ def tile_picked_highway_gelu_l_kernel(tc, xT, res, w1, w2, offs, out):
         products(y_bank, w1b0, 1, 0)
         quant_4b()
         products(y_bank, w1b1, 1, 1)
+        round_w(nc.vector.tensor_copy, w2a1, w2_raw[0], 1)
         round_w(nc.vector.tensor_copy, w2a0, w2_raw[0], 0)
-        round_w(nc.scalar.copy, w2a1, w2_raw[0], 1)
+        quant_5()
         round_w(nc.vector.tensor_copy, w2b0, w2_raw[1], 0)
         round_w(nc.vector.tensor_copy, w2b1, w2_raw[1], 1)
         quant_6()

@@ -22,7 +22,7 @@ BLOCKS = N // P
 HALF = S // 2
 GROUP = 16
 QUARTER = S // 4
-RES_SPLIT = 384
+RES_SPLIT = 320
 
 
 def tile_picked_highway_gelu_l_kernel(tc, xT, res, w1, w2, offs, out):

from contextlib import ExitStack

import concourse.mybir as mybir

K, T, S, N = 1024, 1024, 512, 256
FLOPS = 2 * 2 * K * S * N

F32 = mybir.dt.float32
BF16 = mybir.dt.bfloat16
U32 = mybir.dt.uint32
U16 = mybir.dt.uint16
U8 = mybir.dt.uint8
FP8X4 = mybir.dt.float8_e4m3fn_x4
ACT = mybir.ActivationFunctionType
ALU = mybir.AluOpType

P = 128
PACK = 4
K_PASS = P * PACK
PASSES = K // K_PASS
BLOCKS = N // P
HALF = S // 2
GROUP = 16
QUARTER = S // 4
RES_SPLIT = 320


def tile_picked_highway_gelu_l_kernel(tc, xT, res, w1, w2, offs, out):
    nc = tc.nc
    with ExitStack() as ctx:
        keep = ctx.enter_context(tc.tile_pool(name="keep", bufs=1))
        psum = ctx.enter_context(tc.psum_pool(name="psum", bufs=1))

        def sb(name, shape, dtype, on=None):
            return keep.tile(shape, dtype, name=name, tag=on or name, align_bytes=64)

        offsets = keep.tile([P, S // GROUP], U16, name="offsets")
        warm_in = sb("warm_in", [P, 1], F32)
        warm_out = sb("warm_out", [P, 1], F32)
        nc.vector.memset(warm_in[:], 0.0)
        nc.scalar.activation(warm_out[:], warm_in[:], ACT.Gelu_apprx_tanh)

        all_toks = slice(0, S)
        halves = [slice(h * HALF, (h + 1) * HALF) for h in range(2)]
        blocks = [slice(b * P, (b + 1) * P) for b in range(BLOCKS)]
        quarters = [(b, h) for b in range(BLOCKS) for h in range(2)]

        def cols(first, last):
            return slice(first * HALF, (last + 1) * HALF)

        def entries(toks):
            return offsets[:, toks.start // GROUP : toks.stop // GROUP]

        def pass_rows(src, g):
            return src[g * K_PASS : (g + 1) * K_PASS, :].rearrange("(p t) c -> p t c", t=PACK)

        def load(tile, src):
            nc.sync.dma_start(tile[:], src)
            return tile

        def load_rows(g, first, count):
            tile = sb(f"x_raw{g}{first}", [P, count * T], F32)
            nc.sync.dma_start(
                tile[:].rearrange("p (e c) -> p e c", e=count), pass_rows(xT, g)[:, first : first + count, :]
            )
            return [tile[:, e * T : (e + 1) * T] for e in range(count)]

        x_rows = load_rows(0, 0, 2)
        nc.sync.dma_start(offsets[:], offs)
        x_rows.extend(load_rows(0, 2, 1))
        x_rows.extend(load_rows(0, 3, 1))
        x_rows.extend(load_rows(1, 0, 2))
        x_rows.extend(load_rows(1, 2, 1))
        x_rows.extend(load_rows(1, 3, 1))
        w1_raw = [load(sb(f"w1_raw{g}", [P, PACK, N], F32), pass_rows(w1, g)) for g in range(PASSES)]
        w2_raw = [load(sb(f"w2_raw{g}", [P, PACK, N], F32), pass_rows(w2, g)) for g in range(PASSES)]
        res_raw = [load(sb(f"res_raw{b}", [P, T], F32), res[blocks[b], :]) for b in range(BLOCKS)]

        picked = [sb(f"picked{g}", [P, PACK * S], F32) for g in range(PASSES)]

        def picked_row(row, toks):
            g, t = divmod(row, PACK)
            return picked[g][:, t * S + toks.start : t * S + toks.stop]

        def gather_on_vector(row, toks):
            nc.vector.tensor_copy(picked_row(row, toks), x_rows[row].indirect(entries(toks)))

        def gather_on_scalar(row, toks):
            nc.scalar.activation(picked_row(row, toks), x_rows[row].indirect(entries(toks)), ACT.Copy)

        def batch(name, widths):
            total = sum(widths)
            grouped = sb(name + "_grouped", [P, total, PACK], BF16)
            codes = sb(name + "_codes", [P, total], U32)
            scales = sb(name + "_scales", [P, total], U8)
            starts = [sum(widths[:i]) for i in range(len(widths))]
            parts = [slice(a, a + n) for a, n in zip(starts, widths)]

            def quantise():
                nc.vector.quantize_mx(
                    out=codes[:].bitcast(FP8X4), scales=scales[:], in_=grouped[:].rearrange("p m t -> p (m t)")
                )

            return quantise, [(grouped[:, c, :], codes[:, c].bitcast(FP8X4), scales[:, c]) for c in parts]

        def interleave(copy, dst, src):
            copy(dst.rearrange("p (c i) t -> p c t i", i=4), src.rearrange("p t (c i) -> p c t i", i=4))

        def weave(copy, g, part, first, toks):
            src = picked[g][:].rearrange("p (t s) -> p t s", t=PACK)
            interleave(copy, part[0][:, toks.start - first : toks.stop - first, :], src[:, :, toks])

        def round_w(copy, part, raw, b):
            interleave(copy, part[0], raw[:, :, blocks[b]])

        def multiply(bank, w_part, x_part, g):
            nc.tensor.matmul_mx(
                out=bank[:],
                lhsT=w_part[1],
                lhsT_scale=w_part[2],
                rhs=x_part[1],
                rhs_scale=x_part[2],
                start=(g == 0),
                stop=(g == PASSES - 1),
            )

        y_bank = [psum.tile([P, HALF], F32, name=f"y_bank{i}") for i in range(4)]

        quant_0, (x00,) = batch("q0", [HALF])
        quant_1, (x01,) = batch("q1", [HALF])
        quant_2, (w1a0, x10) = batch("q2", [P, HALF])
        quant_3, (w1a1, x11) = batch("q3", [P, HALF])
        quant_4a, (w1b0,) = batch("q4a", [P])
        quant_4b, (w1b1,) = batch("q4b", [P])
        quant_6, (w2a0, w2b0) = batch("q6", [P, P])
        quant_5, (w2a1,) = batch("q5", [P])
        quant_7, (w2b1,) = batch("q7", [P])
        x_parts = [[x00, x01], [x10, x11]]

        def products(banks, w_part, g, b):
            for h in range(2):
                multiply(banks[2 * b + h], w_part, x_parts[g][h], g)

        def share(row, split):
            gather_on_vector(row, slice(0, split))
            gather_on_scalar(row, slice(split, S))

        def last_row(g, split):
            row = PACK * g + PACK - 1
            gather_on_vector(row, slice(0, QUARTER))
            gather_on_scalar(row, slice(QUARTER, HALF))
            gather_on_scalar(row, halves[1])
            weave(nc.vector.tensor_copy, g, x_parts[g][0], 0, halves[0])
            weave(nc.vector.tensor_copy, g, x_parts[g][1], HALF, slice(HALF, split))
            if split < S:
                weave(nc.scalar.copy, g, x_parts[g][1], HALF, slice(split, S))

        gather_on_vector(0, all_toks)
        gather_on_scalar(1, all_toks)
        share(2, HALF)
        last_row(0, S - QUARTER)
        quant_0()
        quant_1()
        gather_on_vector(4, all_toks)
        gather_on_scalar(5, all_toks)
        share(6, HALF)
        last_row(1, S)

        round_w(nc.scalar.copy, w1a0, w1_raw[0], 0)
        quant_2()
        products(y_bank, w1a0, 0, 0)
        round_w(nc.scalar.copy, w1a1, w1_raw[0], 1)
        quant_3()
        products(y_bank, w1a1, 0, 1)
        round_w(nc.vector.tensor_copy, w1b0, w1_raw[1], 0)
        round_w(nc.scalar.copy, w1b1, w1_raw[1], 1)
        quant_4a()
        products(y_bank, w1b0, 1, 0)
        quant_4b()
        products(y_bank, w1b1, 1, 1)
        round_w(nc.vector.tensor_copy, w2a1, w2_raw[0], 1)
        round_w(nc.vector.tensor_copy, w2a0, w2_raw[0], 0)
        quant_5()
        round_w(nc.vector.tensor_copy, w2b0, w2_raw[1], 0)
        round_w(nc.vector.tensor_copy, w2b1, w2_raw[1], 1)
        quant_6()
        quant_7()
        w2_parts = [[w2a0, w2a1], [w2b0, w2b1]]

        y = sb("y", [P, BLOCKS * S], F32)
        for i in range(4):
            nc.scalar.activation(y[:, cols(i, i)], y_bank[i][:], ACT.Gelu_apprx_tanh)

        r = sb("r", [P, BLOCKS * S], F32)
        d = sb("d", [P, BLOCKS * S], F32)
        o = sb("o", [P, BLOCKS * S], F32)

        def span(b, toks):
            return slice(b * S + toks.start, b * S + toks.stop)

        def window(b, toks):
            return res_raw[b][:].indirect(entries(toks))

        def fused(b, toks):
            nc.vector.tensor_tensor(d[:, span(b, toks)], window(b, toks), y[:, span(b, toks)], ALU.subtract)

        plain = [[slice(RES_SPLIT, S)], halves]
        fused(0, slice(0, RES_SPLIT))
        for b in range(BLOCKS):
            for toks in plain[b]:
                nc.scalar.activation(r[:, span(b, toks)], window(b, toks), ACT.Copy)
        for b in range(BLOCKS):
            g_bank = [psum.tile([P, HALF], F32, name=f"g_bank{b}{h}", tag=f"g_bank{h}") for h in range(2)]
            for h in range(2):
                for g in range(PASSES):
                    multiply(g_bank[h], w2_parts[g][b], x_parts[g][h], g)
            both = [cols(2 * b + h, 2 * b + h) for h in range(2)]
            th = [sb(f"tanh{b}{h}", [P, HALF], F32, on=("tanh01", "e00")[h] if b else None) for h in range(2)]
            for h in range(2):
                nc.scalar.activation(th[h][:], g_bank[h][:], ACT.Tanh, scale=-0.5)
            for toks in plain[b]:
                c = span(b, toks)
                nc.vector.tensor_tensor(d[:, c], r[:, c], y[:, c], ALU.subtract)
            e = [sb(f"e{b}{h}", [P, HALF], F32) for h in range(2)]
            for h in range(2):
                nc.vector.scalar_tensor_tensor(e[h][:], th[h][:], 1.0, d[:, both[h]], ALU.add, ALU.mult)
            for h in range(2):
                nc.vector.scalar_tensor_tensor(o[:, both[h]], e[h][:], 0.5, y[:, both[h]], ALU.mult, ALU.add)
                if b > 0:
                    nc.sync.dma_start(out[blocks[b], halves[h]], o[:, both[h]])
            if b == 0:
                nc.sync.dma_start(out[blocks[b], :], o[:, cols(0, 1)])
